import numpy as np
import ml_dtypes


def mxq(x, axis, fmt="e4m3"):
    dtype, down = {"e4m3": (ml_dtypes.float8_e4m3fn, 7), "e5m2": (ml_dtypes.float8_e5m2, 14)}[fmt]
    v = np.moveaxis(np.asarray(x, np.float32).astype(ml_dtypes.bfloat16).astype(np.float64), axis, -1)
    blocks = v.reshape(v.shape[:-1] + (-1, 32))
    amax = np.abs(blocks).max(-1, keepdims=True)
    byte = np.maximum(np.where(amax > 0, np.frexp(amax)[1] - 1 + 127, 0) - down, 1)
    scale = np.exp2(byte - 127.0)
    codes = (blocks / scale).astype(np.float32).astype(dtype).astype(np.float64)
    return np.moveaxis((codes * scale).reshape(v.shape), -1, axis)


WIDE = False


def mx_kscale(k):
    if not WIDE:
        return np.ones(k)
    levels = np.array([24, -24, 12, -12, 0])
    if k % 512:
        return np.exp2(np.random.permutation(np.resize(levels, k // 32))).repeat(32)
    a = np.empty((k // 512, 16))
    for p in range(k // 512):
        a[p, :8] = np.random.permutation(np.resize(levels, 8))
        for g in range(8):
            far = levels[np.abs(levels - a[p, g]) >= 10]
            a[p, g + 8] = far[np.random.randint(len(far))]
    return np.exp2(a.ravel()).repeat(32)


def f64(x):
    return np.asarray(x).astype(np.float64)


def striped(idx):
    return np.tile(idx.reshape(-1, 16).T, (8, 1)).astype(np.uint16)


def unstriped(offs):
    return offs[:16].T.reshape(-1).astype(np.int64)


def striped8(idx):
    return np.concatenate([v.reshape(-1, 16).T for v in idx]).astype(np.uint16)


def unstriped8(offs):
    return np.stack([offs[16 * g:16 * g + 16].T.reshape(-1) for g in range(8)]).astype(np.int64)


E2M1 = np.array([0.0, 0.5, 1.0, 1.5, 2.0, 3.0, 4.0, 6.0, -0.0, -0.5, -1.0, -1.5, -2.0, -3.0, -4.0, -6.0])


def pack_weight(w, fmt):
    k, n = w.shape
    w = f64(np.asarray(w, np.float32).astype(ml_dtypes.bfloat16)).reshape(k // 32, 32, n)
    amax = np.abs(w).max(1)
    if fmt == "e4m3":
        byte = np.frexp(amax)[1] - 1 + 127 - 7
    else:
        mant, ex = np.frexp(amax / 6.0)
        byte = np.where(mant > 0.5, ex, ex - 1) + 127
    byte = np.clip(np.where(amax > 0, byte, 1), 1, 254)
    scaled = (w * np.exp2(127.0 - byte)[:, None, :]).reshape(k, n).astype(np.float32)
    by_word = np.ascontiguousarray(scaled.reshape(k // 512, 128, 4, n).transpose(0, 1, 3, 2))
    if fmt == "e4m3":
        words = by_word.astype(ml_dtypes.float8_e4m3fn).view(np.uint8)
    else:
        c = by_word.astype(ml_dtypes.float4_e2m1fn).view(np.uint8) & 0xF
        words = (c[..., 0::2] | (c[..., 1::2] << 4)).reshape(k // 512, 128, 2 * n)
    return np.ascontiguousarray(words), np.ascontiguousarray(byte.astype(np.uint8).reshape(k // 512, 16, n))


def unpack_weight(words, scales, fmt):
    g, _, n = scales.shape
    words = np.ascontiguousarray(words).reshape(g, 128, n, -1)
    if fmt == "e4m3":
        vals = words.view(ml_dtypes.float8_e4m3fn).astype(np.float64)
    else:
        nib = np.empty((g, 128, n, 4), np.uint8)
        nib[..., 0::2] = words & 0xF
        nib[..., 1::2] = words >> 4
        vals = E2M1[nib]
    vals = vals * np.repeat(np.exp2(scales.astype(np.float64) - 127.0), 8, axis=1)[..., None]
    return vals.transpose(0, 1, 3, 2).reshape(g * 512, n)


K, L, R, N, T, J = 512, 512, 512, 512, 2048, 1024


def setup_inputs():
    n = np.random.standard_normal
    s = mx_kscale(K)[:, None]
    s2 = mx_kscale(L)[:, None]
    u = mx_kscale(R)[:, None]
    p_tab = pack_weight(n((L, T)) * s2, "e4m3")
    p_wb = pack_weight(n((L, R)) / np.sqrt(L) / s2, "e4m3")
    p_wd = pack_weight(n((R, N)) / np.sqrt(R) / u, "e4m3")
    return {
        "tab_words": p_tab[0],
        "tab_scales": p_tab[1],
        "xT": (n((K, T)) * s).astype(np.float32),
        "wgt2": np.repeat(np.random.uniform(0.5, 2.0, (8, J)), 16, axis=0).astype(np.float32),
        "wa": (n((K, R)) / np.sqrt(K) / s * u.T).astype(np.float32),
        "wb_words": p_wb[0],
        "wb_scales": p_wb[1],
        "wd_words": p_wd[0],
        "wd_scales": p_wd[1],
        "b": (0.3 * n(N)).astype(np.float32),
        "offs": striped(np.random.permutation(T)[:J]),
        "offs2": striped8(np.stack([np.random.permutation(T)[:J] for _ in range(8)])),
    }


def reference(tab_words, tab_scales, xT, wgt2, wa, wb_words, wb_scales, wd_words, wd_scales, b, offs, offs2):
    idx = unstriped(offs)
    idx2 = unstriped8(offs2)
    tab_ = unpack_weight(tab_words, tab_scales, "e4m3")[:, idx]
    rows = np.arange(K)
    xg = f64(wgt2)[rows // 4 % 128] * f64(xT)[rows[:, None], idx2[rows % 512 // 64]]
    xT_ = mxq(xg, 0, "e4m3")
    wa_ = mxq(f64(wa), 0, "e4m3")
    wb_ = unpack_weight(wb_words, wb_scales, "e4m3")
    ya = wa_.T @ xT_
    yb = wb_.T @ tab_
    h = ya * yb
    h_ = mxq(h, 0, "e4m3")
    wd_ = unpack_weight(wd_words, wd_scales, "e4m3")
    y = wd_.T @ h_
    return y + f64(b)[:, None]

@@ -1,0 +1,236 @@
+from contextlib import ExitStack
+
+import concourse.mybir as mybir
+
+K, L, R, N, T, J = 512, 512, 512, 512, 2048, 1024
+FLOPS = 2 * J * (K * R + L * R + R * N)
+
+F32 = mybir.dt.float32
+BF16 = mybir.dt.bfloat16
+I32 = mybir.dt.int32
+U32 = mybir.dt.uint32
+U16 = mybir.dt.uint16
+U8 = mybir.dt.uint8
+FP8X4 = mybir.dt.float8_e4m3fn_x4
+MULT = mybir.AluOpType.mult
+ADD = mybir.AluOpType.add
+IDENTITY = mybir.ActivationFunctionType.Identity
+
+P = 128
+PACK = 4
+SUB = 128
+PARTS = [(0, 256), (256, 1024)]
+CHUNKS = [(0, 256), (256, 512), (512, 768), (768, 896), (896, 1024)]
+
+
+def load_scale_rows(queue, plane, rows, first):
+    for q in range(4):
+        queue.dma_start(
+            out=plane[32 * q + first : 32 * q + first + 4, :].bitcast(I32),
+            in_=rows[0, 4 * q : 4 * q + 4, :].bitcast(I32),
+        )
+
+
+def words_of(packed):
+    return packed[0].rearrange("p c i -> p (c i)").bitcast(I32)
+
+
+def tile_list_htabg_mul_bias_kernel(tc, tab_words, tab_scales, xT, wgt2, wa, wb_words, wb_scales, wd_words, wd_scales, b, offs, offs2, out):
+    nc = tc.nc
+    with ExitStack() as ctx:
+        keep = ctx.enter_context(tc.tile_pool(name="keep", bufs=1))
+        first_psum = ctx.enter_context(tc.psum_pool(name="first_psum", bufs=4))
+        last_psum = ctx.enter_context(tc.psum_pool(name="last_psum", bufs=4))
+
+        tab_list = keep.tile([P, J // 16], U16, name="tab_list")
+        head_lists = keep.tile([P, J // 16], U16, name="head_lists")
+        tab_w = keep.tile([P, T], I32, name="tab_w", tag="slot_a", align_bytes=64)
+        tab_s = keep.tile([P, T], U8, name="tab_s", tag="slot_b", align_bytes=64)
+        wb_w = keep.tile([P, R], I32, name="wb_w", tag="slot_c", align_bytes=64)
+        wb_s = keep.tile([P, R], U8, name="wb_s", tag="slot_d", align_bytes=64)
+        wgt = keep.tile([P, J], F32, name="wgt")
+        x_plane = [keep.tile([P, T], F32, name="x_plane0", tag="slot_e", align_bytes=64)]
+
+        nc.gpsimd.memset(tab_s[:].bitcast(I32), 0)
+        nc.gpsimd.memset(wb_s[:].bitcast(I32), 0)
+
+        x_rows = xT.rearrange("(p i) t -> i p t", i=PACK)
+        wa_rows = wa.rearrange("(p i) r -> p i r", i=PACK)
+        nc.sync.dma_start(tab_list[:], offs)
+        nc.sync.dma_start(head_lists[:], offs2)
+        nc.sync.dma_start(out=tab_w[:], in_=words_of(tab_words))
+        nc.sync.dma_start(out=wb_w[:], in_=words_of(wb_words))
+        nc.sync.dma_start(out=wgt[:], in_=wgt2)
+        nc.sync.dma_start(out=x_plane[0][:], in_=x_rows[0])
+        x_plane.append(keep.tile([P, T], F32, name="x_plane1", tag="slot_h", align_bytes=64))
+        nc.sync.dma_start(out=x_plane[1][:], in_=x_rows[1])
+        load_scale_rows(nc.scalar, tab_s, tab_scales, 0)
+        load_scale_rows(nc.gpsimd, wb_s, wb_scales, 0)
+
+        v_w = keep.tile([P, J], U32, name="v_w", align_bytes=64)
+        nc.vector.tensor_copy(v_w[:], tab_w[:].bitcast(U32).indirect(tab_list[:]))
+        v_s = keep.tile([P, J], U8, name="v_s", tag="slot_a", align_bytes=64)
+        for half in range(2):
+            nc.vector.tensor_copy(
+                v_s[:, half * (J // 2) : (half + 1) * (J // 2)],
+                tab_s[:].indirect(tab_list[:, half * (J // 32) : (half + 1) * (J // 32)]),
+            )
+        wa_raw = keep.tile([P, PACK, R], F32, name="wa_raw", tag="slot_b", align_bytes=64)
+        nc.sync.dma_start(out=wa_raw[:], in_=wa_rows)
+
+        wbp_w = keep.tile([P, R], I32, name="wbp_w", tag="slot_f", align_bytes=64)
+        wbp_s = keep.tile([P, R], U8, name="wbp_s", tag="slot_g", align_bytes=64)
+        nc.vector.tensor_copy(
+            out=wbp_s[:].rearrange("p (t c i) -> p c t i", t=PACK, i=16),
+            in_=wb_s[:].rearrange("p (c i t) -> p c t i", t=PACK, i=16),
+        )
+
+        nc.vector.tensor_copy(
+            out=wbp_w[:].rearrange("p (t c i) -> p c t i", t=PACK, i=4),
+            in_=wb_w[:].rearrange("p (c i t) -> p c t i", t=PACK, i=4),
+        )
+        x_plane.append(keep.tile([P, T], F32, name="x_plane2", tag="slot_c", align_bytes=64))
+        nc.sync.dma_start(out=x_plane[2][:], in_=x_rows[2])
+
+        yb = [keep.tile([P, SUB * PACK], F32, name="yb%d" % s) for s in range(J // SUB)]
+        for s in range(J // SUB):
+            cols = slice(s * SUB, (s + 1) * SUB)
+            acc = first_psum.tile([P, PACK, SUB], F32, name="first_acc")
+            for t in range(PACK):
+                rows = slice(t * P, (t + 1) * P)
+                nc.tensor.matmul_mx(
+                    out=acc[:, t, :],
+                    lhsT=wbp_w[:, rows].bitcast(FP8X4),
+                    lhsT_scale=wbp_s[:, rows],
+                    rhs=v_w[:, cols].bitcast(FP8X4),
+                    rhs_scale=v_s[:, cols],
+                    start=True,
+                    stop=True,
+                )
+            nc.scalar.activation(
+                out=yb[s][:].rearrange("p (n t) -> p n t", t=PACK),
+                in_=acc[:].rearrange("p t n -> p n t"),
+                func=IDENTITY,
+            )
+
+        picked = [
+            keep.tile([P, PACK, hi - lo], F32, name="picked%d" % g, tag=("slot_i", "slot_d")[g], align_bytes=64)
+            for g, (lo, hi) in enumerate(PARTS)
+        ]
+
+        def gather(i):
+            for g, (lo, hi) in enumerate(PARTS):
+                nc.vector.tensor_tensor(
+                    picked[g][:, i, :],
+                    x_plane[i][:].indirect(head_lists[:, lo // 16 : hi // 16]),
+                    wgt[:, lo:hi],
+                    MULT,
+                )
+
+        gather(0)
+        x_plane.append(keep.tile([P, T], F32, name="x_plane3", tag="slot_e", align_bytes=64))
+        nc.sync.dma_start(out=x_plane[3][:], in_=x_rows[3])
+        gather(1)
+        wd_w = keep.tile([P, N], I32, name="wd_w", tag="slot_h", align_bytes=64)
+        nc.sync.dma_start(out=wd_w[:], in_=words_of(wd_words))
+
+        wd_s = keep.tile([P, N], U8, name="wd_s", tag="slot_g", align_bytes=64)
+        load_scale_rows(nc.sync, wd_s, wd_scales, 0)
+        bias = keep.tile([P, N // P], F32, name="bias", tag="slot_f", align_bytes=64)
+        with nc.allow_non_contiguous_dma(reason="one bias value a partition"):
+            nc.sync.dma_start(out=bias[:], in_=b.rearrange("(t p) -> p t", p=P))
+
+        wa_bf = keep.tile([P, R * PACK], BF16, name="wa_bf", align_bytes=64)
+        wa_w = keep.tile([P, R], U32, name="wa_w", align_bytes=64)
+        wa_s = keep.tile([P, R], U8, name="wa_s", align_bytes=64)
+        nc.scalar.copy(
+            out=wa_bf[:].rearrange("p (t m i) -> p m t i", t=PACK, i=PACK),
+            in_=wa_raw[:].rearrange("p i (m t) -> p m t i", t=PACK),
+        )
+        nc.vector.quantize_mx(out=wa_w[:].bitcast(FP8X4), scales=wa_s[:], in_=wa_bf[:])
+
+        gather(2)
+        gather(3)
+
+        x_bf = [keep.tile([P, (hi - lo) * PACK], BF16, name="x_bf%d" % c, align_bytes=64) for c, (lo, hi) in enumerate(CHUNKS)]
+        x_w = [keep.tile([P, hi - lo], U32, name="x_w%d" % c, align_bytes=64) for c, (lo, hi) in enumerate(CHUNKS)]
+        x_s = [keep.tile([P, hi - lo], U8, name="x_s%d" % c, align_bytes=64) for c, (lo, hi) in enumerate(CHUNKS)]
+        h_bf = [keep.tile([P, (hi - lo) * PACK], BF16, name="h_bf%d" % c, align_bytes=64) for c, (lo, hi) in enumerate(CHUNKS)]
+        h_w = [keep.tile([P, hi - lo], U32, name="h_w%d" % c, align_bytes=64) for c, (lo, hi) in enumerate(CHUNKS)]
+        h_s = [keep.tile([P, hi - lo], U8, name="h_s%d" % c, align_bytes=64) for c, (lo, hi) in enumerate(CHUNKS)]
+        result = [keep.tile([P, N // P, hi - lo], F32, name="result%d" % c) for c, (lo, hi) in enumerate(CHUNKS)]
+        out_rows = out.rearrange("(t p) j -> p t j", p=P)
+        ya = {}
+
+        def pick_last_plane(c):
+            lo, hi = CHUNKS[c]
+            g = min(c, len(PARTS) - 1)
+            first = PARTS[g][0]
+            nc.scalar.copy(
+                out=x_bf[c][:].rearrange("p (c i t) -> p c t i", t=PACK, i=4),
+                in_=picked[g][:, :, lo - first : hi - first].rearrange("p t (c i) -> p c t i", i=4),
+            )
+
+        def first_layer(c):
+            lo, hi = CHUNKS[c]
+            nc.vector.quantize_mx(out=x_w[c][:].bitcast(FP8X4), scales=x_s[c][:], in_=x_bf[c][:])
+            for s in range(lo // SUB, hi // SUB):
+                cols = slice(s * SUB - lo, (s + 1) * SUB - lo)
+                ya[s] = first_psum.tile([P, PACK, SUB], F32, name="first_acc")
+                for t in range(PACK):
+                    rows = slice(t * P, (t + 1) * P)
+                    nc.tensor.matmul_mx(
+                        out=ya[s][:, t, :],
+                        lhsT=wa_w[:, rows].bitcast(FP8X4),
+                        lhsT_scale=wa_s[:, rows],
+                        rhs=x_w[c][:, cols].bitcast(FP8X4),
+                        rhs_scale=x_s[c][:, cols],
+                        start=True,
+                        stop=True,
+                    )
+
+        def product(c):
+            lo, hi = CHUNKS[c]
+            for s in range(lo // SUB, hi // SUB):
+                cols = slice((s * SUB - lo) * PACK, ((s + 1) * SUB - lo) * PACK)
+                nc.vector.tensor_tensor(
+                    h_bf[c][:, cols].rearrange("p (n t) -> p n t", t=PACK),
+                    ya[s][:].rearrange("p t n -> p n t"),
+                    yb[s][:].rearrange("p (n t) -> p n t", t=PACK),
+                    MULT,
+                )
+
+        def second_layer(c):
+            lo, hi = CHUNKS[c]
+            nc.vector.quantize_mx(out=h_w[c][:].bitcast(FP8X4), scales=h_s[c][:], in_=h_bf[c][:])
+            for u in range(2):
+                acc = last_psum.tile([P, 2, hi - lo], F32, name="last_acc")
+                for v in range(2):
+                    rows = slice((2 * u + v) * P, (2 * u + v + 1) * P)
+                    nc.tensor.matmul_mx(
+                        out=acc[:, v, :],
+                        lhsT=wd_w[:, rows].bitcast(FP8X4),
+                        lhsT_scale=wd_s[:, rows],
+                        rhs=h_w[c][:].bitcast(FP8X4),
+                        rhs_scale=h_s[c][:],
+                        start=True,
+                        stop=True,
+                    )
+                for v in range(2):
+                    t = 2 * u + v
+                    if c == len(CHUNKS) - 1 and u == 1:
+                        nc.vector.tensor_scalar(result[c][:, t, :], acc[:, v, :], bias[:, t : t + 1], None, ADD)
+                    else:
+                        nc.scalar.activation(out=result[c][:, t, :], in_=acc[:, v, :], func=IDENTITY, bias=bias[:, t : t + 1])
+            nc.sync.dma_start(out=out_rows[:, :, lo:hi], in_=result[c][:])
+
+        n = len(CHUNKS)
+        for step in range(n + 2):
+            if step < n:
+                pick_last_plane(step)
+            if 0 <= step - 1 < n:
+                first_layer(step - 1)
+            if 0 <= step - 2 < n:
+                product(step - 2)
+            if 0 <= step - 2 < n:
+                second_layer(step - 2)

@@ -20,6 +20,7 @@ P = 128
 PACK = 4
 SUB = 128
 PARTS = [(0, 256), (256, 1024)]
+WB_PARTS = [(0, 128), (128, 256), (256, 384), (384, 512)]
 CHUNKS = [(0, 256), (256, 512), (512, 768), (768, 896), (896, 1024)]
 
 
@@ -46,50 +47,58 @@ def tile_list_htabg_mul_bias_kernel(tc, tab_words, tab_scales, xT, wgt2, wa, wb_
         head_lists = keep.tile([P, J // 16], U16, name="head_lists")
         tab_w = keep.tile([P, T], I32, name="tab_w", tag="slot_a", align_bytes=64)
         tab_s = keep.tile([P, T], U8, name="tab_s", tag="slot_b", align_bytes=64)
-        wb_w = keep.tile([P, R], I32, name="wb_w", tag="slot_c", align_bytes=64)
-        wb_s = keep.tile([P, R], U8, name="wb_s", tag="slot_d", align_bytes=64)
+        wb_w = [
+            keep.tile([P, hi - lo], I32, name="wb_w%d" % g, tag=("slot_e", "slot_c", "slot_d", "slot_g")[g], align_bytes=64)
+            for g, (lo, hi) in enumerate(WB_PARTS)
+        ]
         wgt = keep.tile([P, J], F32, name="wgt")
-        x_plane = [keep.tile([P, T], F32, name="x_plane0", tag="slot_e", align_bytes=64)]
 
         nc.gpsimd.memset(tab_s[:].bitcast(I32), 0)
-        nc.gpsimd.memset(wb_s[:].bitcast(I32), 0)
 
         x_rows = xT.rearrange("(p i) t -> i p t", i=PACK)
         wa_rows = wa.rearrange("(p i) r -> p i r", i=PACK)
         nc.sync.dma_start(tab_list[:], offs)
-        nc.sync.dma_start(head_lists[:], offs2)
+        for g, (lo, hi) in enumerate(WB_PARTS):
+            nc.sync.dma_start(out=wb_w[g][:], in_=words_of(wb_words)[:, lo:hi])
         nc.sync.dma_start(out=tab_w[:], in_=words_of(tab_words))
-        nc.sync.dma_start(out=wb_w[:], in_=words_of(wb_words))
+        nc.sync.dma_start(head_lists[:], offs2)
         nc.sync.dma_start(out=wgt[:], in_=wgt2)
+        load_scale_rows(nc.sync, tab_s, tab_scales, 0)
+
+        wbp_w = keep.tile([P, R], I32, name="wbp_w", tag="slot_f", align_bytes=64)
+
+        def reorder_wb_words(g):
+            lo, hi = WB_PARTS[g]
+            nc.vector.tensor_copy(
+                out=wbp_w[:].rearrange("p (t c i) -> p c t i", t=PACK, i=4)[:, lo // 16 : hi // 16],
+                in_=wb_w[g][:].rearrange("p (c i t) -> p c t i", t=PACK, i=4),
+            )
+
+        reorder_wb_words(0)
+        reorder_wb_words(1)
+        x_plane = [keep.tile([P, T], F32, name="x_plane0", tag="slot_c", align_bytes=64)]
         nc.sync.dma_start(out=x_plane[0][:], in_=x_rows[0])
-        x_plane.append(keep.tile([P, T], F32, name="x_plane1", tag="slot_h", align_bytes=64))
+        wb_s = keep.tile([P, R], U8, name="wb_s", tag="slot_e", align_bytes=64)
+        nc.vector.memset(wb_s[:].bitcast(I32), 0)
+        load_scale_rows(nc.sync, wb_s, wb_scales, 0)
+        reorder_wb_words(2)
+        reorder_wb_words(3)
+        wa_raw = keep.tile([P, PACK, R], F32, name="wa_raw", tag="slot_d", align_bytes=64)
+        nc.sync.dma_start(out=wa_raw[:], in_=wa_rows)
+        x_plane.append(keep.tile([P, T], F32, name="x_plane1", tag="slot_g", align_bytes=64))
         nc.sync.dma_start(out=x_plane[1][:], in_=x_rows[1])
-        load_scale_rows(nc.scalar, tab_s, tab_scales, 0)
-        load_scale_rows(nc.gpsimd, wb_s, wb_scales, 0)
 
         v_w = keep.tile([P, J], U32, name="v_w", align_bytes=64)
         nc.vector.tensor_copy(v_w[:], tab_w[:].bitcast(U32).indirect(tab_list[:]))
         v_s = keep.tile([P, J], U8, name="v_s", tag="slot_a", align_bytes=64)
-        for half in range(2):
-            nc.vector.tensor_copy(
-                v_s[:, half * (J // 2) : (half + 1) * (J // 2)],
-                tab_s[:].indirect(tab_list[:, half * (J // 32) : (half + 1) * (J // 32)]),
-            )
-        wa_raw = keep.tile([P, PACK, R], F32, name="wa_raw", tag="slot_b", align_bytes=64)
-        nc.sync.dma_start(out=wa_raw[:], in_=wa_rows)
+        nc.vector.tensor_copy(v_s[:], tab_s[:].indirect(tab_list[:]))
 
-        wbp_w = keep.tile([P, R], I32, name="wbp_w", tag="slot_f", align_bytes=64)
-        wbp_s = keep.tile([P, R], U8, name="wbp_s", tag="slot_g", align_bytes=64)
+        wbp_s = keep.tile([P, R], U8, name="wbp_s", tag="slot_h", align_bytes=64)
         nc.vector.tensor_copy(
             out=wbp_s[:].rearrange("p (t c i) -> p c t i", t=PACK, i=16),
             in_=wb_s[:].rearrange("p (c i t) -> p c t i", t=PACK, i=16),
         )
-
-        nc.vector.tensor_copy(
-            out=wbp_w[:].rearrange("p (t c i) -> p c t i", t=PACK, i=4),
-            in_=wb_w[:].rearrange("p (c i t) -> p c t i", t=PACK, i=4),
-        )
-        x_plane.append(keep.tile([P, T], F32, name="x_plane2", tag="slot_c", align_bytes=64))
+        x_plane.append(keep.tile([P, T], F32, name="x_plane2", tag="slot_b", align_bytes=64))
         nc.sync.dma_start(out=x_plane[2][:], in_=x_rows[2])
 
         yb = [keep.tile([P, SUB * PACK], F32, name="yb%d" % s) for s in range(J // SUB)]
@@ -114,7 +123,7 @@ def tile_list_htabg_mul_bias_kernel(tc, tab_words, tab_scales, xT, wgt2, wa, wb_
             )
 
         picked = [
-            keep.tile([P, PACK, hi - lo], F32, name="picked%d" % g, tag=("slot_i", "slot_d")[g], align_bytes=64)
+            keep.tile([P, PACK, hi - lo], F32, name="picked%d" % g, tag=("slot_i", "slot_e")[g], align_bytes=64)
             for g, (lo, hi) in enumerate(PARTS)
         ]
 
@@ -128,29 +137,31 @@ def tile_list_htabg_mul_bias_kernel(tc, tab_words, tab_scales, xT, wgt2, wa, wb_
                 )
 
         gather(0)
-        x_plane.append(keep.tile([P, T], F32, name="x_plane3", tag="slot_e", align_bytes=64))
-        nc.sync.dma_start(out=x_plane[3][:], in_=x_rows[3])
-        gather(1)
-        wd_w = keep.tile([P, N], I32, name="wd_w", tag="slot_h", align_bytes=64)
-        nc.sync.dma_start(out=wd_w[:], in_=words_of(wd_words))
 
-        wd_s = keep.tile([P, N], U8, name="wd_s", tag="slot_g", align_bytes=64)
+        wa_bf = keep.tile([P, R * PACK], BF16, name="wa_bf", align_bytes=64)
+        wa_s = keep.tile([P, R], U8, name="wa_s", align_bytes=64)
+        nc.scalar.activation(
+            out=wa_bf[:].rearrange("p (t m i) -> p m t i", t=PACK, i=PACK),
+            in_=wa_raw[:].rearrange("p i (m t) -> p m t i", t=PACK),
+            func=IDENTITY,
+        )
+
+        x_plane.append(keep.tile([P, T], F32, name="x_plane3", tag="slot_c", align_bytes=64))
+        nc.sync.dma_start(out=x_plane[3][:], in_=x_rows[3])
+
+        gather(1)
+        wd_w = keep.tile([P, N], I32, name="wd_w", tag="slot_g", align_bytes=64)
+        nc.sync.dma_start(out=wd_w[:], in_=words_of(wd_words))
+        wd_s = keep.tile([P, N], U8, name="wd_s", tag="slot_h", align_bytes=64)
         load_scale_rows(nc.sync, wd_s, wd_scales, 0)
         bias = keep.tile([P, N // P], F32, name="bias", tag="slot_f", align_bytes=64)
         with nc.allow_non_contiguous_dma(reason="one bias value a partition"):
             nc.sync.dma_start(out=bias[:], in_=b.rearrange("(t p) -> p t", p=P))
 
-        wa_bf = keep.tile([P, R * PACK], BF16, name="wa_bf", align_bytes=64)
-        wa_w = keep.tile([P, R], U32, name="wa_w", align_bytes=64)
-        wa_s = keep.tile([P, R], U8, name="wa_s", align_bytes=64)
-        nc.scalar.copy(
-            out=wa_bf[:].rearrange("p (t m i) -> p m t i", t=PACK, i=PACK),
-            in_=wa_raw[:].rearrange("p i (m t) -> p m t i", t=PACK),
-        )
-        nc.vector.quantize_mx(out=wa_w[:].bitcast(FP8X4), scales=wa_s[:], in_=wa_bf[:])
-
         gather(2)
         gather(3)
+        wa_w = keep.tile([P, R], U32, name="wa_w", tag="slot_c", align_bytes=64)
+        nc.vector.quantize_mx(out=wa_w[:].bitcast(FP8X4), scales=wa_s[:], in_=wa_bf[:])
 
         x_bf = [keep.tile([P, (hi - lo) * PACK], BF16, name="x_bf%d" % c, align_bytes=64) for c, (lo, hi) in enumerate(CHUNKS)]
         x_w = [keep.tile([P, hi - lo], U32, name="x_w%d" % c, align_bytes=64) for c, (lo, hi) in enumerate(CHUNKS)]

@@ -21,7 +21,8 @@ PACK = 4
 SUB = 128
 PARTS = [(0, 256), (256, 1024)]
 WB_PARTS = [(0, 128), (128, 256), (256, 384), (384, 512)]
-CHUNKS = [(0, 256), (256, 512), (512, 768), (768, 896), (896, 1024)]
+FIRST = [(0, 256), (256, 512), (512, 768), (768, 1024)]
+SECOND = [(0, 256), (256, 512), (512, 768), (768, 896), (896, 1024)]
 
 
 def load_scale_rows(queue, plane, rows, first):
@@ -48,7 +49,7 @@ def tile_list_htabg_mul_bias_kernel(tc, tab_words, tab_scales, xT, wgt2, wa, wb_
         tab_w = keep.tile([P, T], I32, name="tab_w", tag="slot_a", align_bytes=64)
         tab_s = keep.tile([P, T], U8, name="tab_s", tag="slot_b", align_bytes=64)
         wb_w = [
-            keep.tile([P, hi - lo], I32, name="wb_w%d" % g, tag=("slot_e", "slot_c", "slot_d", "slot_g")[g], align_bytes=64)
+            keep.tile([P, hi - lo], I32, name="wb_w%d" % g, tag=("slot_d", "slot_c", "slot_e", "slot_g")[g], align_bytes=64)
             for g, (lo, hi) in enumerate(WB_PARTS)
         ]
         wgt = keep.tile([P, J], F32, name="wgt")
@@ -74,19 +75,34 @@ def tile_list_htabg_mul_bias_kernel(tc, tab_words, tab_scales, xT, wgt2, wa, wb_
                 in_=wb_w[g][:].rearrange("p (c i t) -> p c t i", t=PACK, i=4),
             )
 
+        def load_wa_half(h, tag):
+            half = keep.tile([P, PACK, R // 2], F32, name="wa_raw%d" % h, tag=tag, align_bytes=64)
+            nc.sync.dma_start(out=half[:], in_=wa_rows[:, :, h * (R // 2) : (h + 1) * (R // 2)])
+            return half
+
         reorder_wb_words(0)
+        wa_raw = [load_wa_half(0, "slot_d")]
         reorder_wb_words(1)
         x_plane = [keep.tile([P, T], F32, name="x_plane0", tag="slot_c", align_bytes=64)]
         nc.sync.dma_start(out=x_plane[0][:], in_=x_rows[0])
+        reorder_wb_words(2)
         wb_s = keep.tile([P, R], U8, name="wb_s", tag="slot_e", align_bytes=64)
         nc.vector.memset(wb_s[:].bitcast(I32), 0)
         load_scale_rows(nc.sync, wb_s, wb_scales, 0)
-        reorder_wb_words(2)
         reorder_wb_words(3)
-        wa_raw = keep.tile([P, PACK, R], F32, name="wa_raw", tag="slot_d", align_bytes=64)
-        nc.sync.dma_start(out=wa_raw[:], in_=wa_rows)
         x_plane.append(keep.tile([P, T], F32, name="x_plane1", tag="slot_g", align_bytes=64))
         nc.sync.dma_start(out=x_plane[1][:], in_=x_rows[1])
+
+        wa_bf = keep.tile([P, R * PACK], BF16, name="wa_bf", align_bytes=64)
+
+        def interleave_wa_half(h):
+            nc.scalar.activation(
+                out=wa_bf[:].rearrange("p (t m i) -> p m t i", t=PACK, i=PACK)[:, h * 64 : (h + 1) * 64],
+                in_=wa_raw[h][:].rearrange("p i (m t) -> p m t i", t=PACK),
+                func=IDENTITY,
+            )
+
+        interleave_wa_half(0)
 
         v_w = keep.tile([P, J], U32, name="v_w", align_bytes=64)
         nc.vector.tensor_copy(v_w[:], tab_w[:].bitcast(U32).indirect(tab_list[:]))
@@ -98,7 +114,8 @@ def tile_list_htabg_mul_bias_kernel(tc, tab_words, tab_scales, xT, wgt2, wa, wb_
             out=wbp_s[:].rearrange("p (t c i) -> p c t i", t=PACK, i=16),
             in_=wb_s[:].rearrange("p (c i t) -> p c t i", t=PACK, i=16),
         )
-        x_plane.append(keep.tile([P, T], F32, name="x_plane2", tag="slot_b", align_bytes=64))
+        wa_raw.append(load_wa_half(1, "slot_b"))
+        x_plane.append(keep.tile([P, T], F32, name="x_plane2", tag="slot_d", align_bytes=64))
         nc.sync.dma_start(out=x_plane[2][:], in_=x_rows[2])
 
         yb = [keep.tile([P, SUB * PACK], F32, name="yb%d" % s) for s in range(J // SUB)]
@@ -117,8 +134,8 @@ def tile_list_htabg_mul_bias_kernel(tc, tab_words, tab_scales, xT, wgt2, wa, wb_
                     stop=True,
                 )
             nc.scalar.activation(
-                out=yb[s][:].rearrange("p (n t) -> p n t", t=PACK),
-                in_=acc[:].rearrange("p t n -> p n t"),
+                out=yb[s][:].rearrange("p (c t i) -> p c t i", t=PACK, i=4),
+                in_=acc[:].rearrange("p t (c i) -> p c t i", i=4),
                 func=IDENTITY,
             )
 
@@ -138,13 +155,8 @@ def tile_list_htabg_mul_bias_kernel(tc, tab_words, tab_scales, xT, wgt2, wa, wb_
 
         gather(0)
 
-        wa_bf = keep.tile([P, R * PACK], BF16, name="wa_bf", align_bytes=64)
         wa_s = keep.tile([P, R], U8, name="wa_s", align_bytes=64)
-        nc.scalar.activation(
-            out=wa_bf[:].rearrange("p (t m i) -> p m t i", t=PACK, i=PACK),
-            in_=wa_raw[:].rearrange("p i (m t) -> p m t i", t=PACK),
-            func=IDENTITY,
-        )
+        interleave_wa_half(1)
 
         x_plane.append(keep.tile([P, T], F32, name="x_plane3", tag="slot_c", align_bytes=64))
         nc.sync.dma_start(out=x_plane[3][:], in_=x_rows[3])
@@ -163,18 +175,17 @@ def tile_list_htabg_mul_bias_kernel(tc, tab_words, tab_scales, xT, wgt2, wa, wb_
         wa_w = keep.tile([P, R], U32, name="wa_w", tag="slot_c", align_bytes=64)
         nc.vector.quantize_mx(out=wa_w[:].bitcast(FP8X4), scales=wa_s[:], in_=wa_bf[:])
 
-        x_bf = [keep.tile([P, (hi - lo) * PACK], BF16, name="x_bf%d" % c, align_bytes=64) for c, (lo, hi) in enumerate(CHUNKS)]
-        x_w = [keep.tile([P, hi - lo], U32, name="x_w%d" % c, align_bytes=64) for c, (lo, hi) in enumerate(CHUNKS)]
-        x_s = [keep.tile([P, hi - lo], U8, name="x_s%d" % c, align_bytes=64) for c, (lo, hi) in enumerate(CHUNKS)]
-        h_bf = [keep.tile([P, (hi - lo) * PACK], BF16, name="h_bf%d" % c, align_bytes=64) for c, (lo, hi) in enumerate(CHUNKS)]
-        h_w = [keep.tile([P, hi - lo], U32, name="h_w%d" % c, align_bytes=64) for c, (lo, hi) in enumerate(CHUNKS)]
-        h_s = [keep.tile([P, hi - lo], U8, name="h_s%d" % c, align_bytes=64) for c, (lo, hi) in enumerate(CHUNKS)]
-        result = [keep.tile([P, N // P, hi - lo], F32, name="result%d" % c) for c, (lo, hi) in enumerate(CHUNKS)]
+        x_bf = [keep.tile([P, (hi - lo) * PACK], BF16, name="x_bf%d" % c, align_bytes=64) for c, (lo, hi) in enumerate(FIRST)]
+        x_w = [keep.tile([P, hi - lo], U32, name="x_w%d" % c, align_bytes=64) for c, (lo, hi) in enumerate(FIRST)]
+        x_s = [keep.tile([P, hi - lo], U8, name="x_s%d" % c, align_bytes=64) for c, (lo, hi) in enumerate(FIRST)]
+        h_bf = [keep.tile([P, (hi - lo) * PACK], BF16, name="h_bf%d" % c, align_bytes=64) for c, (lo, hi) in enumerate(SECOND)]
+        h_w = [keep.tile([P, hi - lo], U32, name="h_w%d" % c, align_bytes=64) for c, (lo, hi) in enumerate(SECOND)]
+        h_s = [keep.tile([P, hi - lo], U8, name="h_s%d" % c, align_bytes=64) for c, (lo, hi) in enumerate(SECOND)]
         out_rows = out.rearrange("(t p) j -> p t j", p=P)
         ya = {}
 
-        def pick_last_plane(c):
-            lo, hi = CHUNKS[c]
+        def interleave_x(c):
+            lo, hi = FIRST[c]
             g = min(c, len(PARTS) - 1)
             first = PARTS[g][0]
             nc.scalar.copy(
@@ -183,7 +194,7 @@ def tile_list_htabg_mul_bias_kernel(tc, tab_words, tab_scales, xT, wgt2, wa, wb_
             )
 
         def first_layer(c):
-            lo, hi = CHUNKS[c]
+            lo, hi = FIRST[c]
             nc.vector.quantize_mx(out=x_w[c][:].bitcast(FP8X4), scales=x_s[c][:], in_=x_bf[c][:])
             for s in range(lo // SUB, hi // SUB):
                 cols = slice(s * SUB - lo, (s + 1) * SUB - lo)
@@ -201,19 +212,21 @@ def tile_list_htabg_mul_bias_kernel(tc, tab_words, tab_scales, xT, wgt2, wa, wb_
                     )
 
         def product(c):
-            lo, hi = CHUNKS[c]
+            lo, hi = SECOND[c]
             for s in range(lo // SUB, hi // SUB):
                 cols = slice((s * SUB - lo) * PACK, ((s + 1) * SUB - lo) * PACK)
                 nc.vector.tensor_tensor(
-                    h_bf[c][:, cols].rearrange("p (n t) -> p n t", t=PACK),
-                    ya[s][:].rearrange("p t n -> p n t"),
-                    yb[s][:].rearrange("p (n t) -> p n t", t=PACK),
+                    h_bf[c][:, cols].rearrange("p (c i t) -> p c t i", t=PACK, i=4),
+                    ya[s][:].rearrange("p t (c i) -> p c t i", i=4),
+                    yb[s][:].rearrange("p (c t i) -> p c t i", t=PACK, i=4),
                     MULT,
                 )
 
         def second_layer(c):
-            lo, hi = CHUNKS[c]
+            lo, hi = SECOND[c]
+            last = c == len(SECOND) - 1
             nc.vector.quantize_mx(out=h_w[c][:].bitcast(FP8X4), scales=h_s[c][:], in_=h_bf[c][:])
+            result = keep.tile([P, N // P, hi - lo], F32, name="result%d" % c)
             for u in range(2):
                 acc = last_psum.tile([P, 2, hi - lo], F32, name="last_acc")
                 for v in range(2):
@@ -229,19 +242,23 @@ def tile_list_htabg_mul_bias_kernel(tc, tab_words, tab_scales, xT, wgt2, wa, wb_
                     )
                 for v in range(2):
                     t = 2 * u + v
-                    if c == len(CHUNKS) - 1 and u == 1:
-                        nc.vector.tensor_scalar(result[c][:, t, :], acc[:, v, :], bias[:, t : t + 1], None, ADD)
+                    if last and u == 1:
+                        nc.vector.tensor_scalar(result[:, t, :], acc[:, v, :], bias[:, t : t + 1], None, ADD)
                     else:
-                        nc.scalar.activation(out=result[c][:, t, :], in_=acc[:, v, :], func=IDENTITY, bias=bias[:, t : t + 1])
-            nc.sync.dma_start(out=out_rows[:, :, lo:hi], in_=result[c][:])
+                        nc.scalar.activation(out=result[:, t, :], in_=acc[:, v, :], func=IDENTITY, bias=bias[:, t : t + 1])
+                if last:
+                    queue = (nc.scalar, nc.sync)[u]
+                    queue.dma_start(out=out_rows[:, 2 * u : 2 * u + 2, lo:hi], in_=result[:, 2 * u : 2 * u + 2, :])
+            if not last:
+                nc.sync.dma_start(out=out_rows[:, :, lo:hi], in_=result[:])
 
-        n = len(CHUNKS)
-        for step in range(n + 2):
-            if step < n:
-                pick_last_plane(step)
-            if 0 <= step - 1 < n:
-                first_layer(step - 1)
-            if 0 <= step - 2 < n:
-                product(step - 2)
-            if 0 <= step - 2 < n:
-                second_layer(step - 2)
+        for c in range(len(FIRST)):
+            interleave_x(c)
+        first_layer(0)
+        for c in range(len(SECOND) + 1):
+            if c + 1 < len(FIRST):
+                first_layer(c + 1)
+            if c >= 1:
+                second_layer(c - 1)
+            if c < len(SECOND):
+                product(c)

@@ -1,6 +1,7 @@
 from contextlib import ExitStack
 
 import concourse.mybir as mybir
+from concourse.masks import make_identity
 
 K, L, R, N, T, J = 512, 512, 512, 512, 2048, 1024
 FLOPS = 2 * J * (K * R + L * R + R * N)
@@ -19,17 +20,19 @@ IDENTITY = mybir.ActivationFunctionType.Identity
 P = 128
 PACK = 4
 SUB = 128
-PARTS = [(0, 256), (256, 1024)]
-WB_PARTS = [(0, 128), (128, 256), (256, 384), (384, 512)]
+STAGE = 112
+HEADS = 8
+RUN = J // P
+PARTS = [(0, 256), (256, 512), (512, 1024)]
 FIRST = [(0, 256), (256, 512), (512, 768), (768, 1024)]
 SECOND = [(0, 256), (256, 512), (512, 768), (768, 896), (896, 1024)]
 
 
-def load_scale_rows(queue, plane, rows, first):
+def place_scale_rows(queue, plane, rows):
     for q in range(4):
         queue.dma_start(
-            out=plane[32 * q + first : 32 * q + first + 4, :].bitcast(I32),
-            in_=rows[0, 4 * q : 4 * q + 4, :].bitcast(I32),
+            out=plane[32 * q : 32 * q + 4, :].bitcast(I32),
+            in_=rows[4 * q : 4 * q + 4, :].bitcast(I32),
         )
 
 
@@ -44,56 +47,32 @@ def tile_list_htabg_mul_bias_kernel(tc, tab_words, tab_scales, xT, wgt2, wa, wb_
         first_psum = ctx.enter_context(tc.psum_pool(name="first_psum", bufs=4))
         last_psum = ctx.enter_context(tc.psum_pool(name="last_psum", bufs=4))
 
+        def tile(shape, dtype, name, slot=""):
+            return keep.tile(shape, dtype, name=name, tag=slot or name, align_bytes=64)
+
         tab_list = keep.tile([P, J // 16], U16, name="tab_list")
         head_lists = keep.tile([P, J // 16], U16, name="head_lists")
-        tab_w = keep.tile([P, T], I32, name="tab_w", tag="slot_a", align_bytes=64)
-        tab_s = keep.tile([P, T], U8, name="tab_s", tag="slot_b", align_bytes=64)
-        wb_w = [
-            keep.tile([P, hi - lo], I32, name="wb_w%d" % g, tag=("slot_d", "slot_c", "slot_e", "slot_g")[g], align_bytes=64)
-            for g, (lo, hi) in enumerate(WB_PARTS)
-        ]
-        wgt = keep.tile([P, J], F32, name="wgt")
-
-        nc.gpsimd.memset(tab_s[:].bitcast(I32), 0)
-
+        tab_s = tile([P, T], U8, "tab_s", "slot_a")
+        tab_w = tile([P, T], I32, "tab_w", "slot_b")
+        wb_w = tile([P, R], I32, "wb_w")
+        wb_s = tile([P, R], U8, "wb_s")
+        wgt = tile([P, J], F32, "wgt")
         x_rows = xT.rearrange("(p i) t -> i p t", i=PACK)
         wa_rows = wa.rearrange("(p i) r -> p i r", i=PACK)
-        nc.sync.dma_start(tab_list[:], offs)
-        for g, (lo, hi) in enumerate(WB_PARTS):
-            nc.sync.dma_start(out=wb_w[g][:], in_=words_of(wb_words)[:, lo:hi])
-        nc.sync.dma_start(out=tab_w[:], in_=words_of(tab_words))
-        nc.sync.dma_start(head_lists[:], offs2)
-        nc.sync.dma_start(out=wgt[:], in_=wgt2)
-        load_scale_rows(nc.sync, tab_s, tab_scales, 0)
 
-        wbp_w = keep.tile([P, R], I32, name="wbp_w", tag="slot_f", align_bytes=64)
+        for staged in (tab_s, wb_s):
+            nc.vector.memset(staged[0:96, :].bitcast(I32), 0)
+            nc.vector.memset(staged[96:STAGE, :].bitcast(I32), 0)
 
-        def reorder_wb_words(g):
-            lo, hi = WB_PARTS[g]
-            nc.vector.tensor_copy(
-                out=wbp_w[:].rearrange("p (t c i) -> p c t i", t=PACK, i=4)[:, lo // 16 : hi // 16],
-                in_=wb_w[g][:].rearrange("p (c i t) -> p c t i", t=PACK, i=4),
-            )
+        identity = tile([P, P], F32, "identity")
+        make_identity(nc, identity[:])
 
-        def load_wa_half(h, tag):
-            half = keep.tile([P, PACK, R // 2], F32, name="wa_raw%d" % h, tag=tag, align_bytes=64)
+        def load_wa_half(h, slot):
+            half = tile([P, PACK, R // 2], F32, "wa_raw%d" % h, slot)
             nc.sync.dma_start(out=half[:], in_=wa_rows[:, :, h * (R // 2) : (h + 1) * (R // 2)])
             return half
 
-        reorder_wb_words(0)
-        wa_raw = [load_wa_half(0, "slot_d")]
-        reorder_wb_words(1)
-        x_plane = [keep.tile([P, T], F32, name="x_plane0", tag="slot_c", align_bytes=64)]
-        nc.sync.dma_start(out=x_plane[0][:], in_=x_rows[0])
-        reorder_wb_words(2)
-        wb_s = keep.tile([P, R], U8, name="wb_s", tag="slot_e", align_bytes=64)
-        nc.vector.memset(wb_s[:].bitcast(I32), 0)
-        load_scale_rows(nc.sync, wb_s, wb_scales, 0)
-        reorder_wb_words(3)
-        x_plane.append(keep.tile([P, T], F32, name="x_plane1", tag="slot_g", align_bytes=64))
-        nc.sync.dma_start(out=x_plane[1][:], in_=x_rows[1])
-
-        wa_bf = keep.tile([P, R * PACK], BF16, name="wa_bf", align_bytes=64)
+        wa_bf = tile([P, R * PACK], BF16, "wa_bf")
 
         def interleave_wa_half(h):
             nc.scalar.activation(
@@ -102,23 +81,63 @@ def tile_list_htabg_mul_bias_kernel(tc, tab_words, tab_scales, xT, wgt2, wa, wb_
                 func=IDENTITY,
             )
 
+        head_w = tile([P, HEADS, RUN], F32, "head_w")
+        nc.sync.dma_start(tab_list[:], offs)
+        nc.sync.dma_start(out=tab_s[STAGE:P, :].bitcast(I32), in_=tab_scales[0].bitcast(I32))
+        nc.sync.dma_start(out=wb_s[STAGE:P, :].bitcast(I32), in_=wb_scales[0].bitcast(I32))
+        nc.sync.dma_start(out=head_w[:], in_=wgt2.rearrange("(g s) (q c) -> s q g c", s=16, c=RUN)[0])
+        nc.sync.dma_start(head_lists[:], offs2)
+        nc.sync.dma_start(out=tab_w[:], in_=words_of(tab_words))
+        nc.sync.dma_start(out=wb_w[:], in_=words_of(wb_words))
+        wa_raw = [load_wa_half(0, "slot_f")]
+        x_plane = [tile([P, T], F32, "x_plane0", "slot_e")]
+        nc.sync.dma_start(out=x_plane[0][:], in_=x_rows[0])
+
+        spread = tile([P, RUN, P], F32, "spread")
+        nc.scalar.copy(
+            out=spread[:].rearrange("q c (g s) -> q c g s", s=16),
+            in_=head_w[:].rearrange("q g c -> q c g").unsqueeze(3).to_broadcast([P, RUN, HEADS, 16]),
+        )
+        for u in range(RUN // PACK):
+            turned = first_psum.tile([P, PACK, SUB], F32, name="first_acc")
+            for c in range(PACK):
+                nc.tensor.transpose(turned[:, c, :], spread[:, PACK * u + c, :], identity[:])
+            nc.scalar.copy(
+                out=wgt[:].rearrange("p (q u c) -> p u q c", u=RUN // PACK, c=PACK)[:, u],
+                in_=turned[:].rearrange("p c q -> p q c"),
+            )
         interleave_wa_half(0)
 
-        v_w = keep.tile([P, J], U32, name="v_w", align_bytes=64)
-        nc.vector.tensor_copy(v_w[:], tab_w[:].bitcast(U32).indirect(tab_list[:]))
-        v_s = keep.tile([P, J], U8, name="v_s", tag="slot_a", align_bytes=64)
-        nc.vector.tensor_copy(v_s[:], tab_s[:].indirect(tab_list[:]))
-
-        wbp_s = keep.tile([P, R], U8, name="wbp_s", tag="slot_h", align_bytes=64)
+        v_rows = tile([P, J], U8, "v_rows", "slot_g")
+        nc.vector.tensor_copy(v_rows[:], tab_s[:].indirect(tab_list[:]))
+        both_rows = tile([P, J + R], U8, "both_rows", "slot_c")
         nc.vector.tensor_copy(
-            out=wbp_s[:].rearrange("p (t c i) -> p c t i", t=PACK, i=16),
+            out=both_rows[:, J:].rearrange("p (t c i) -> p c t i", t=PACK, i=16),
             in_=wb_s[:].rearrange("p (c i t) -> p c t i", t=PACK, i=16),
         )
-        wa_raw.append(load_wa_half(1, "slot_b"))
-        x_plane.append(keep.tile([P, T], F32, name="x_plane2", tag="slot_d", align_bytes=64))
+        nc.vector.tensor_copy(both_rows[96:P, :J].bitcast(I32), v_rows[96:P, :].bitcast(I32))
+        both_s = tile([P, J + R], U8, "both_s")
+        place_scale_rows(nc.sync, both_s, both_rows[STAGE:P, :])
+        v_s = both_s[:, :J]
+        wbp_s = both_s[:, J:]
+        x_plane.append(tile([P, T], F32, "x_plane1", "slot_g"))
+        nc.sync.dma_start(out=x_plane[1][:], in_=x_rows[1])
+
+        v_w = tile([P, J], U32, "v_w")
+        nc.vector.tensor_copy(v_w[:], tab_w[:].bitcast(U32).indirect(tab_list[:]))
+        x_plane.append(tile([P, T], F32, "x_plane2", "slot_b"))
         nc.sync.dma_start(out=x_plane[2][:], in_=x_rows[2])
 
-        yb = [keep.tile([P, SUB * PACK], F32, name="yb%d" % s) for s in range(J // SUB)]
+        wbp_w = tile([P, R], I32, "wbp_w")
+        nc.vector.tensor_copy(
+            out=wbp_w[:].rearrange("p (t c i) -> p c t i", t=PACK, i=4),
+            in_=wb_w[:].rearrange("p (c i t) -> p c t i", t=PACK, i=4),
+        )
+
+        wa_raw.append(load_wa_half(1, "slot_f"))
+        interleave_wa_half(1)
+
+        yb = [tile([P, SUB * PACK], F32, "yb%d" % s) for s in range(J // SUB)]
         for s in range(J // SUB):
             cols = slice(s * SUB, (s + 1) * SUB)
             acc = first_psum.tile([P, PACK, SUB], F32, name="first_acc")
@@ -134,63 +153,55 @@ def tile_list_htabg_mul_bias_kernel(tc, tab_words, tab_scales, xT, wgt2, wa, wb_
                     stop=True,
                 )
             nc.scalar.activation(
-                out=yb[s][:].rearrange("p (c t i) -> p c t i", t=PACK, i=4),
-                in_=acc[:].rearrange("p t (c i) -> p c t i", i=4),
+                out=yb[s][:].rearrange("p (c t) -> p c t", t=PACK),
+                in_=acc[:].rearrange("p t c -> p c t"),
                 func=IDENTITY,
             )
 
-        picked = [
-            keep.tile([P, PACK, hi - lo], F32, name="picked%d" % g, tag=("slot_i", "slot_e")[g], align_bytes=64)
-            for g, (lo, hi) in enumerate(PARTS)
-        ]
+        picked = tile([P, PACK * J], F32, "picked")
 
         def gather(i):
-            for g, (lo, hi) in enumerate(PARTS):
+            for lo, hi in PARTS if i == PACK - 1 else [(0, J)]:
                 nc.vector.tensor_tensor(
-                    picked[g][:, i, :],
+                    picked[:, i * J + lo : i * J + hi],
                     x_plane[i][:].indirect(head_lists[:, lo // 16 : hi // 16]),
                     wgt[:, lo:hi],
                     MULT,
                 )
 
         gather(0)
-
-        wa_s = keep.tile([P, R], U8, name="wa_s", align_bytes=64)
-        interleave_wa_half(1)
-
-        x_plane.append(keep.tile([P, T], F32, name="x_plane3", tag="slot_c", align_bytes=64))
+        x_plane.append(tile([P, T], F32, "x_plane3", "slot_c"))
         nc.sync.dma_start(out=x_plane[3][:], in_=x_rows[3])
-
         gather(1)
-        wd_w = keep.tile([P, N], I32, name="wd_w", tag="slot_g", align_bytes=64)
+        wd_w = tile([P, N], I32, "wd_w", "slot_g")
         nc.sync.dma_start(out=wd_w[:], in_=words_of(wd_words))
-        wd_s = keep.tile([P, N], U8, name="wd_s", tag="slot_h", align_bytes=64)
-        load_scale_rows(nc.sync, wd_s, wd_scales, 0)
-        bias = keep.tile([P, N // P], F32, name="bias", tag="slot_f", align_bytes=64)
+        gather(2)
+        bias = tile([P, N // P], F32, "bias", "slot_b")
         with nc.allow_non_contiguous_dma(reason="one bias value a partition"):
             nc.sync.dma_start(out=bias[:], in_=b.rearrange("(t p) -> p t", p=P))
 
-        gather(2)
-        gather(3)
-        wa_w = keep.tile([P, R], U32, name="wa_w", tag="slot_c", align_bytes=64)
+        wd_s = tile([P, N], U8, "wd_s", "slot_e")
+        place_scale_rows(nc.sync, wd_s, wd_scales[0])
+        wa_s = tile([P, R], U8, "wa_s")
+        wa_w = tile([P, R], U32, "wa_w")
         nc.vector.quantize_mx(out=wa_w[:].bitcast(FP8X4), scales=wa_s[:], in_=wa_bf[:])
 
-        x_bf = [keep.tile([P, (hi - lo) * PACK], BF16, name="x_bf%d" % c, align_bytes=64) for c, (lo, hi) in enumerate(FIRST)]
-        x_w = [keep.tile([P, hi - lo], U32, name="x_w%d" % c, align_bytes=64) for c, (lo, hi) in enumerate(FIRST)]
-        x_s = [keep.tile([P, hi - lo], U8, name="x_s%d" % c, align_bytes=64) for c, (lo, hi) in enumerate(FIRST)]
-        h_bf = [keep.tile([P, (hi - lo) * PACK], BF16, name="h_bf%d" % c, align_bytes=64) for c, (lo, hi) in enumerate(SECOND)]
-        h_w = [keep.tile([P, hi - lo], U32, name="h_w%d" % c, align_bytes=64) for c, (lo, hi) in enumerate(SECOND)]
-        h_s = [keep.tile([P, hi - lo], U8, name="h_s%d" % c, align_bytes=64) for c, (lo, hi) in enumerate(SECOND)]
+        gather(3)
+
+        x_bf = [tile([P, (hi - lo) * PACK], BF16, "x_bf%d" % c) for c, (lo, hi) in enumerate(FIRST)]
+        x_w = [tile([P, hi - lo], U32, "x_w%d" % c) for c, (lo, hi) in enumerate(FIRST)]
+        x_s = [tile([P, hi - lo], U8, "x_s%d" % c) for c, (lo, hi) in enumerate(FIRST)]
+        h_bf = [tile([P, (hi - lo) * PACK], BF16, "h_bf%d" % c) for c, (lo, hi) in enumerate(SECOND)]
+        h_w = [tile([P, hi - lo], U32, "h_w%d" % c) for c, (lo, hi) in enumerate(SECOND)]
+        h_s = [tile([P, hi - lo], U8, "h_s%d" % c) for c, (lo, hi) in enumerate(SECOND)]
         out_rows = out.rearrange("(t p) j -> p t j", p=P)
         ya = {}
 
         def interleave_x(c):
             lo, hi = FIRST[c]
-            g = min(c, len(PARTS) - 1)
-            first = PARTS[g][0]
             nc.scalar.copy(
                 out=x_bf[c][:].rearrange("p (c i t) -> p c t i", t=PACK, i=4),
-                in_=picked[g][:, :, lo - first : hi - first].rearrange("p t (c i) -> p c t i", i=4),
+                in_=picked[:].rearrange("p (t c i) -> p c t i", t=PACK, i=4)[:, lo // 4 : hi // 4],
             )
 
         def first_layer(c):
@@ -216,9 +227,9 @@ def tile_list_htabg_mul_bias_kernel(tc, tab_words, tab_scales, xT, wgt2, wa, wb_
             for s in range(lo // SUB, hi // SUB):
                 cols = slice((s * SUB - lo) * PACK, ((s + 1) * SUB - lo) * PACK)
                 nc.vector.tensor_tensor(
-                    h_bf[c][:, cols].rearrange("p (c i t) -> p c t i", t=PACK, i=4),
-                    ya[s][:].rearrange("p t (c i) -> p c t i", i=4),
-                    yb[s][:].rearrange("p (c t i) -> p c t i", t=PACK, i=4),
+                    h_bf[c][:, cols].rearrange("p (c t) -> p c t", t=PACK),
+                    ya[s][:].rearrange("p t c -> p c t"),
+                    yb[s][:].rearrange("p (c t) -> p c t", t=PACK),
                     MULT,
                 )
 
@@ -226,7 +237,7 @@ def tile_list_htabg_mul_bias_kernel(tc, tab_words, tab_scales, xT, wgt2, wa, wb_
             lo, hi = SECOND[c]
             last = c == len(SECOND) - 1
             nc.vector.quantize_mx(out=h_w[c][:].bitcast(FP8X4), scales=h_s[c][:], in_=h_bf[c][:])
-            result = keep.tile([P, N // P, hi - lo], F32, name="result%d" % c)
+            result = tile([P, N // P, hi - lo], F32, "result%d" % c)
             for u in range(2):
                 acc = last_psum.tile([P, 2, hi - lo], F32, name="last_acc")
                 for v in range(2):

@@ -30,10 +30,7 @@ SECOND = [(0, 256), (256, 512), (512, 768), (768, 896), (896, 1024)]
 
 def place_scale_rows(queue, plane, rows):
     for q in range(4):
-        queue.dma_start(
-            out=plane[32 * q : 32 * q + 4, :].bitcast(I32),
-            in_=rows[4 * q : 4 * q + 4, :].bitcast(I32),
-        )
+        queue.dma_start(out=plane[q:P:32, :].bitcast(I32), in_=rows[q:16:4, :].bitcast(I32))
 
 
 def words_of(packed):
@@ -44,8 +41,7 @@ def tile_list_htabg_mul_bias_kernel(tc, tab_words, tab_scales, xT, wgt2, wa, wb_
     nc = tc.nc
     with ExitStack() as ctx:
         keep = ctx.enter_context(tc.tile_pool(name="keep", bufs=1))
-        first_psum = ctx.enter_context(tc.psum_pool(name="first_psum", bufs=4))
-        last_psum = ctx.enter_context(tc.psum_pool(name="last_psum", bufs=4))
+        psum = ctx.enter_context(tc.psum_pool(name="psum", bufs=8))
 
         def tile(shape, dtype, name, slot=""):
             return keep.tile(shape, dtype, name=name, tag=slot or name, align_bytes=64)
@@ -76,8 +72,8 @@ def tile_list_htabg_mul_bias_kernel(tc, tab_words, tab_scales, xT, wgt2, wa, wb_
 
         def interleave_wa_half(h):
             nc.scalar.activation(
-                out=wa_bf[:].rearrange("p (t m i) -> p m t i", t=PACK, i=PACK)[:, h * 64 : (h + 1) * 64],
-                in_=wa_raw[h][:].rearrange("p i (m t) -> p m t i", t=PACK),
+                out=wa_bf[:].rearrange("p (t m i) -> p m i t", t=PACK, i=PACK)[:, h * 64 : (h + 1) * 64],
+                in_=wa_raw[h][:].rearrange("p i (m t) -> p m i t", t=PACK),
                 func=IDENTITY,
             )
 
@@ -89,9 +85,9 @@ def tile_list_htabg_mul_bias_kernel(tc, tab_words, tab_scales, xT, wgt2, wa, wb_
         nc.sync.dma_start(head_lists[:], offs2)
         nc.sync.dma_start(out=tab_w[:], in_=words_of(tab_words))
         nc.sync.dma_start(out=wb_w[:], in_=words_of(wb_words))
-        wa_raw = [load_wa_half(0, "slot_f")]
         x_plane = [tile([P, T], F32, "x_plane0", "slot_e")]
         nc.sync.dma_start(out=x_plane[0][:], in_=x_rows[0])
+        wa_raw = [load_wa_half(0, "slot_f")]
 
         spread = tile([P, RUN, P], F32, "spread")
         nc.scalar.copy(
@@ -99,7 +95,7 @@ def tile_list_htabg_mul_bias_kernel(tc, tab_words, tab_scales, xT, wgt2, wa, wb_
             in_=head_w[:].rearrange("q g c -> q c g").unsqueeze(3).to_broadcast([P, RUN, HEADS, 16]),
         )
         for u in range(RUN // PACK):
-            turned = first_psum.tile([P, PACK, SUB], F32, name="first_acc")
+            turned = psum.tile([P, PACK, SUB], F32, name="bank")
             for c in range(PACK):
                 nc.tensor.transpose(turned[:, c, :], spread[:, PACK * u + c, :], identity[:])
             nc.scalar.copy(
@@ -134,13 +130,11 @@ def tile_list_htabg_mul_bias_kernel(tc, tab_words, tab_scales, xT, wgt2, wa, wb_
             in_=wb_w[:].rearrange("p (c i t) -> p c t i", t=PACK, i=4),
         )
 
-        wa_raw.append(load_wa_half(1, "slot_f"))
-        interleave_wa_half(1)
 
         yb = [tile([P, SUB * PACK], F32, "yb%d" % s) for s in range(J // SUB)]
         for s in range(J // SUB):
             cols = slice(s * SUB, (s + 1) * SUB)
-            acc = first_psum.tile([P, PACK, SUB], F32, name="first_acc")
+            acc = psum.tile([P, PACK, SUB], F32, name="bank")
             for t in range(PACK):
                 rows = slice(t * P, (t + 1) * P)
                 nc.tensor.matmul_mx(
@@ -169,9 +163,10 @@ def tile_list_htabg_mul_bias_kernel(tc, tab_words, tab_scales, xT, wgt2, wa, wb_
                     MULT,
                 )
 
-        gather(0)
-        x_plane.append(tile([P, T], F32, "x_plane3", "slot_c"))
+        x_plane.append(tile([P, T], F32, "x_plane3", "slot_f"))
         nc.sync.dma_start(out=x_plane[3][:], in_=x_rows[3])
+        wa_raw.append(load_wa_half(1, "slot_c"))
+        gather(0)
         gather(1)
         wd_w = tile([P, N], I32, "wd_w", "slot_g")
         nc.sync.dma_start(out=wd_w[:], in_=words_of(wd_words))
@@ -182,11 +177,11 @@ def tile_list_htabg_mul_bias_kernel(tc, tab_words, tab_scales, xT, wgt2, wa, wb_
 
         wd_s = tile([P, N], U8, "wd_s", "slot_e")
         place_scale_rows(nc.sync, wd_s, wd_scales[0])
+        gather(3)
+        interleave_wa_half(1)
         wa_s = tile([P, R], U8, "wa_s")
         wa_w = tile([P, R], U32, "wa_w")
         nc.vector.quantize_mx(out=wa_w[:].bitcast(FP8X4), scales=wa_s[:], in_=wa_bf[:])
-
-        gather(3)
 
         x_bf = [tile([P, (hi - lo) * PACK], BF16, "x_bf%d" % c) for c, (lo, hi) in enumerate(FIRST)]
         x_w = [tile([P, hi - lo], U32, "x_w%d" % c) for c, (lo, hi) in enumerate(FIRST)]
@@ -209,7 +204,7 @@ def tile_list_htabg_mul_bias_kernel(tc, tab_words, tab_scales, xT, wgt2, wa, wb_
             nc.vector.quantize_mx(out=x_w[c][:].bitcast(FP8X4), scales=x_s[c][:], in_=x_bf[c][:])
             for s in range(lo // SUB, hi // SUB):
                 cols = slice(s * SUB - lo, (s + 1) * SUB - lo)
-                ya[s] = first_psum.tile([P, PACK, SUB], F32, name="first_acc")
+                ya[s] = psum.tile([P, PACK, SUB], F32, name="bank")
                 for t in range(PACK):
                     rows = slice(t * P, (t + 1) * P)
                     nc.tensor.matmul_mx(
@@ -222,28 +217,28 @@ def tile_list_htabg_mul_bias_kernel(tc, tab_words, tab_scales, xT, wgt2, wa, wb_
                         stop=True,
                     )
 
-        def product(c):
-            lo, hi = SECOND[c]
-            for s in range(lo // SUB, hi // SUB):
-                cols = slice((s * SUB - lo) * PACK, ((s + 1) * SUB - lo) * PACK)
-                nc.vector.tensor_tensor(
-                    h_bf[c][:, cols].rearrange("p (c t) -> p c t", t=PACK),
-                    ya[s][:].rearrange("p t c -> p c t"),
-                    yb[s][:].rearrange("p (c t) -> p c t", t=PACK),
-                    MULT,
-                )
+        def product(s):
+            c = max(k for k, chunk in enumerate(SECOND) if chunk[0] <= s * SUB)
+            first = (s * SUB - SECOND[c][0]) * PACK
+            nc.vector.tensor_tensor(
+                h_bf[c][:, first : first + SUB * PACK].rearrange("p (c t) -> p c t", t=PACK),
+                ya[s][:].rearrange("p t c -> p c t"),
+                yb[s][:].rearrange("p (c t) -> p c t", t=PACK),
+                MULT,
+            )
+
+        y = {}
+        result = [tile([P, N // P, hi - lo], F32, "result%d" % c) for c, (lo, hi) in enumerate(SECOND)]
 
         def second_layer(c):
             lo, hi = SECOND[c]
-            last = c == len(SECOND) - 1
             nc.vector.quantize_mx(out=h_w[c][:].bitcast(FP8X4), scales=h_s[c][:], in_=h_bf[c][:])
-            result = tile([P, N // P, hi - lo], F32, "result%d" % c)
             for u in range(2):
-                acc = last_psum.tile([P, 2, hi - lo], F32, name="last_acc")
+                y[c, u] = psum.tile([P, 2, hi - lo], F32, name="bank")
                 for v in range(2):
                     rows = slice((2 * u + v) * P, (2 * u + v + 1) * P)
                     nc.tensor.matmul_mx(
-                        out=acc[:, v, :],
+                        out=y[c, u][:, v, :],
                         lhsT=wd_w[:, rows].bitcast(FP8X4),
                         lhsT_scale=wd_s[:, rows],
                         rhs=h_w[c][:].bitcast(FP8X4),
@@ -251,25 +246,43 @@ def tile_list_htabg_mul_bias_kernel(tc, tab_words, tab_scales, xT, wgt2, wa, wb_
                         start=True,
                         stop=True,
                     )
-                for v in range(2):
-                    t = 2 * u + v
-                    if last and u == 1:
-                        nc.vector.tensor_scalar(result[:, t, :], acc[:, v, :], bias[:, t : t + 1], None, ADD)
-                    else:
-                        nc.scalar.activation(out=result[:, t, :], in_=acc[:, v, :], func=IDENTITY, bias=bias[:, t : t + 1])
-                if last:
-                    queue = (nc.scalar, nc.sync)[u]
-                    queue.dma_start(out=out_rows[:, 2 * u : 2 * u + 2, lo:hi], in_=result[:, 2 * u : 2 * u + 2, :])
-            if not last:
-                nc.sync.dma_start(out=out_rows[:, :, lo:hi], in_=result[:])
 
+        def empty_on_scalar(c, u):
+            for v in range(2):
+                t = 2 * u + v
+                nc.scalar.activation(out=result[c][:, t, :], in_=y[c, u][:, v, :], func=IDENTITY, bias=bias[:, t : t + 1])
+
+        def empty_on_vector(c, u):
+            lo, hi = SECOND[c]
+            pair = slice(2 * u, 2 * u + 2)
+            nc.vector.tensor_tensor(result[c][:, pair, :], y[c, u][:], bias[:, pair].unsqueeze(2).to_broadcast([P, 2, hi - lo]), ADD)
+
+        def store(queue, c, slices):
+            lo, hi = SECOND[c]
+            queue.dma_start(out=out_rows[:, slices, lo:hi], in_=result[c][:, slices, :])
+
+        last = len(SECOND) - 1
         for c in range(len(FIRST)):
             interleave_x(c)
         first_layer(0)
-        for c in range(len(SECOND) + 1):
-            if c + 1 < len(FIRST):
-                first_layer(c + 1)
-            if c >= 1:
-                second_layer(c - 1)
-            if c < len(SECOND):
-                product(c)
+        first_layer(1)
+        for s in range(J // SUB):
+            product(s)
+            for c, (lo, hi) in enumerate(FIRST[2:], 2):
+                if lo == (s + 3) * SUB:
+                    first_layer(c)
+            for c, (lo, hi) in enumerate(SECOND):
+                if hi == s * SUB:
+                    second_layer(c)
+                    empty_on_scalar(c, 0)
+                    store(nc.sync, c, slice(0, 2))
+                    if c < last - 1:
+                        empty_on_scalar(c, 1)
+                        store(nc.sync, c, slice(2, 4))
+        second_layer(last)
+        empty_on_scalar(last, 0)
+        empty_on_vector(last - 1, 1)
+        store(nc.sync, last - 1, slice(2, 4))
+        store(nc.scalar, last, slice(0, 2))
+        empty_on_vector(last, 1)
+        store(nc.sync, last, slice(2, 4))

@@ -107,7 +107,7 @@ def tile_list_htabg_mul_bias_kernel(tc, tab_words, tab_scales, xT, wgt2, wa, wb_
         v_rows = tile([P, J], U8, "v_rows", "slot_g")
         nc.vector.tensor_copy(v_rows[:], tab_s[:].indirect(tab_list[:]))
         both_rows = tile([P, J + R], U8, "both_rows", "slot_c")
-        nc.vector.tensor_copy(
+        nc.gpsimd.tensor_copy(
             out=both_rows[:, J:].rearrange("p (t c i) -> p c t i", t=PACK, i=16),
             in_=wb_s[:].rearrange("p (c i t) -> p c t i", t=PACK, i=16),
         )
@@ -125,7 +125,7 @@ def tile_list_htabg_mul_bias_kernel(tc, tab_words, tab_scales, xT, wgt2, wa, wb_
         nc.sync.dma_start(out=x_plane[2][:], in_=x_rows[2])
 
         wbp_w = tile([P, R], I32, "wbp_w")
-        nc.vector.tensor_copy(
+        nc.gpsimd.tensor_copy(
             out=wbp_w[:].rearrange("p (t c i) -> p c t i", t=PACK, i=4),
             in_=wb_w[:].rearrange("p (c i t) -> p c t i", t=PACK, i=4),
         )

@@ -23,6 +23,7 @@ SUB = 128
 STAGE = 112
 HEADS = 8
 RUN = J // P
+WA_SCALAR = 48
 PARTS = [(0, 256), (256, 512), (512, 1024)]
 FIRST = [(0, 256), (256, 512), (512, 768), (768, 1024)]
 SECOND = [(0, 256), (256, 512), (512, 768), (768, 896), (896, 1024)]
@@ -50,7 +51,7 @@ def tile_list_htabg_mul_bias_kernel(tc, tab_words, tab_scales, xT, wgt2, wa, wb_
         head_lists = keep.tile([P, J // 16], U16, name="head_lists")
         tab_s = tile([P, T], U8, "tab_s", "slot_a")
         tab_w = tile([P, T], I32, "tab_w", "slot_b")
-        wb_w = tile([P, R], I32, "wb_w")
+        wb_w = tile([P, R], I32, "wb_w", "slot_f")
         wb_s = tile([P, R], U8, "wb_s")
         wgt = tile([P, J], F32, "wgt")
         x_rows = xT.rearrange("(p i) t -> i p t", i=PACK)
@@ -63,48 +64,42 @@ def tile_list_htabg_mul_bias_kernel(tc, tab_words, tab_scales, xT, wgt2, wa, wb_
         identity = tile([P, P], F32, "identity")
         make_identity(nc, identity[:])
 
-        def load_wa_half(h, slot):
-            half = tile([P, PACK, R // 2], F32, "wa_raw%d" % h, slot)
-            nc.sync.dma_start(out=half[:], in_=wa_rows[:, :, h * (R // 2) : (h + 1) * (R // 2)])
-            return half
-
         wa_bf = tile([P, R * PACK], BF16, "wa_bf")
 
-        def interleave_wa_half(h):
-            nc.scalar.activation(
-                out=wa_bf[:].rearrange("p (t m i) -> p m i t", t=PACK, i=PACK)[:, h * 64 : (h + 1) * 64],
-                in_=wa_raw[h][:].rearrange("p i (m t) -> p m i t", t=PACK),
-                func=IDENTITY,
+        def interleave_wa(copy, share):
+            copy(
+                out=wa_bf[:].rearrange("p (t m i) -> p m i t", t=PACK, i=PACK)[:, share],
+                in_=wa_raw[:].rearrange("p i (m t) -> p m i t", t=PACK)[:, share],
             )
 
-        head_w = tile([P, HEADS, RUN], F32, "head_w")
+        head_w = tile([P, P], F32, "head_w")
+        nc.gpsimd.memset(head_w[HEADS * RUN :, :], 0.0)
         nc.sync.dma_start(tab_list[:], offs)
         nc.sync.dma_start(out=tab_s[STAGE:P, :].bitcast(I32), in_=tab_scales[0].bitcast(I32))
         nc.sync.dma_start(out=wb_s[STAGE:P, :].bitcast(I32), in_=wb_scales[0].bitcast(I32))
-        nc.sync.dma_start(out=head_w[:], in_=wgt2.rearrange("(g s) (q c) -> s q g c", s=16, c=RUN)[0])
+        nc.sync.dma_start(out=head_w[: HEADS * RUN, :], in_=wgt2.rearrange("(g s) (u v) -> s g u v", s=16, v=P)[0])
         nc.sync.dma_start(head_lists[:], offs2)
         nc.sync.dma_start(out=tab_w[:], in_=words_of(tab_words))
         nc.sync.dma_start(out=wb_w[:], in_=words_of(wb_words))
         x_plane = [tile([P, T], F32, "x_plane0", "slot_e")]
         nc.sync.dma_start(out=x_plane[0][:], in_=x_rows[0])
-        wa_raw = [load_wa_half(0, "slot_f")]
+        x_plane.append(tile([P, T], F32, "x_plane1", "slot_g"))
+        nc.sync.dma_start(out=x_plane[1][:], in_=x_rows[1])
 
         spread = tile([P, RUN, P], F32, "spread")
+        by_token = psum.tile([P, P], F32, name="bank")
+        nc.tensor.transpose(by_token[:], head_w[:], identity[:])
         nc.scalar.copy(
-            out=spread[:].rearrange("q c (g s) -> q c g s", s=16),
-            in_=head_w[:].rearrange("q g c -> q c g").unsqueeze(3).to_broadcast([P, RUN, HEADS, 16]),
+            out=spread[:].rearrange("v u (g s) -> v u g s", s=16),
+            in_=by_token[:, : HEADS * RUN].rearrange("v (g u) -> v u g", u=RUN).unsqueeze(3).to_broadcast([P, RUN, HEADS, 16]),
         )
         for u in range(RUN // PACK):
             turned = psum.tile([P, PACK, SUB], F32, name="bank")
             for c in range(PACK):
                 nc.tensor.transpose(turned[:, c, :], spread[:, PACK * u + c, :], identity[:])
-            nc.scalar.copy(
-                out=wgt[:].rearrange("p (q u c) -> p u q c", u=RUN // PACK, c=PACK)[:, u],
-                in_=turned[:].rearrange("p c q -> p q c"),
-            )
-        interleave_wa_half(0)
+            nc.scalar.copy(out=wgt[:, u * PACK * P : (u + 1) * PACK * P], in_=turned[:].rearrange("p c v -> p (c v)"))
 
-        v_rows = tile([P, J], U8, "v_rows", "slot_g")
+        v_rows = tile([P, J], U8, "v_rows")
         nc.vector.tensor_copy(v_rows[:], tab_s[:].indirect(tab_list[:]))
         both_rows = tile([P, J + R], U8, "both_rows", "slot_c")
         nc.gpsimd.tensor_copy(
@@ -116,8 +111,6 @@ def tile_list_htabg_mul_bias_kernel(tc, tab_words, tab_scales, xT, wgt2, wa, wb_
         place_scale_rows(nc.sync, both_s, both_rows[STAGE:P, :])
         v_s = both_s[:, :J]
         wbp_s = both_s[:, J:]
-        x_plane.append(tile([P, T], F32, "x_plane1", "slot_g"))
-        nc.sync.dma_start(out=x_plane[1][:], in_=x_rows[1])
 
         v_w = tile([P, J], U32, "v_w")
         nc.vector.tensor_copy(v_w[:], tab_w[:].bitcast(U32).indirect(tab_list[:]))
@@ -165,20 +158,21 @@ def tile_list_htabg_mul_bias_kernel(tc, tab_words, tab_scales, xT, wgt2, wa, wb_
 
         x_plane.append(tile([P, T], F32, "x_plane3", "slot_f"))
         nc.sync.dma_start(out=x_plane[3][:], in_=x_rows[3])
-        wa_raw.append(load_wa_half(1, "slot_c"))
+        wa_raw = tile([P, PACK, R], F32, "wa_raw", "slot_c")
+        nc.sync.dma_start(out=wa_raw[:], in_=wa_rows)
         gather(0)
         gather(1)
-        wd_w = tile([P, N], I32, "wd_w", "slot_g")
-        nc.sync.dma_start(out=wd_w[:], in_=words_of(wd_words))
         gather(2)
-        bias = tile([P, N // P], F32, "bias", "slot_b")
+        wd_w = tile([P, N], I32, "wd_w", "slot_b")
+        nc.sync.dma_start(out=wd_w[:], in_=words_of(wd_words))
+        bias = tile([P, N // P], F32, "bias", "slot_g")
         with nc.allow_non_contiguous_dma(reason="one bias value a partition"):
             nc.sync.dma_start(out=bias[:], in_=b.rearrange("(t p) -> p t", p=P))
-
-        wd_s = tile([P, N], U8, "wd_s", "slot_e")
-        place_scale_rows(nc.sync, wd_s, wd_scales[0])
         gather(3)
-        interleave_wa_half(1)
+        wd_s = tile([P, N], U8, "wd_s", "slot_f")
+        place_scale_rows(nc.sync, wd_s, wd_scales[0])
+        interleave_wa(nc.scalar.copy, slice(0, WA_SCALAR))
+        interleave_wa(nc.vector.tensor_copy, slice(WA_SCALAR, P))
         wa_s = tile([P, R], U8, "wa_s")
         wa_w = tile([P, R], U32, "wa_w")
         nc.vector.quantize_mx(out=wa_w[:].bitcast(FP8X4), scales=wa_s[:], in_=wa_bf[:])

@@ -23,7 +23,6 @@ SUB = 128
 STAGE = 112
 HEADS = 8
 RUN = J // P
-WA_SCALAR = 48
 PARTS = [(0, 256), (256, 512), (512, 1024)]
 FIRST = [(0, 256), (256, 512), (512, 768), (768, 1024)]
 SECOND = [(0, 256), (256, 512), (512, 768), (768, 896), (896, 1024)]
@@ -57,19 +56,18 @@ def tile_list_htabg_mul_bias_kernel(tc, tab_words, tab_scales, xT, wgt2, wa, wb_
         x_rows = xT.rearrange("(p i) t -> i p t", i=PACK)
         wa_rows = wa.rearrange("(p i) r -> p i r", i=PACK)
 
-        for staged in (tab_s, wb_s):
-            nc.vector.memset(staged[0:96, :].bitcast(I32), 0)
-            nc.vector.memset(staged[96:STAGE, :].bitcast(I32), 0)
+        nc.vector.memset(tab_s[:STAGE, :].bitcast(I32), 0)
+        nc.gpsimd.memset(wb_s[:STAGE, :].bitcast(I32), 0)
 
         identity = tile([P, P], F32, "identity")
         make_identity(nc, identity[:])
 
-        wa_bf = tile([P, R * PACK], BF16, "wa_bf")
+        wa_bf = [tile([P, R * PACK // 2], BF16, "wa_bf%d" % h) for h in range(2)]
 
-        def interleave_wa(copy, share):
+        def interleave_wa(copy, h):
             copy(
-                out=wa_bf[:].rearrange("p (t m i) -> p m i t", t=PACK, i=PACK)[:, share],
-                in_=wa_raw[:].rearrange("p i (m t) -> p m i t", t=PACK)[:, share],
+                out=wa_bf[h][:].rearrange("p (t m i) -> p m i t", t=2, i=PACK),
+                in_=wa_raw[:].rearrange("p i (m t) -> p m i t", t=PACK)[:, :, :, 2 * h : 2 * h + 2],
             )
 
         head_w = tile([P, P], F32, "head_w")
@@ -171,13 +169,8 @@ def tile_list_htabg_mul_bias_kernel(tc, tab_words, tab_scales, xT, wgt2, wa, wb_
         gather(3)
         wd_s = tile([P, N], U8, "wd_s", "slot_f")
         place_scale_rows(nc.sync, wd_s, wd_scales[0])
-        interleave_wa(nc.scalar.copy, slice(0, WA_SCALAR))
-        interleave_wa(nc.vector.tensor_copy, slice(WA_SCALAR, P))
-        wa_s = tile([P, R], U8, "wa_s")
-        wa_w = tile([P, R], U32, "wa_w")
-        nc.vector.quantize_mx(out=wa_w[:].bitcast(FP8X4), scales=wa_s[:], in_=wa_bf[:])
 
-        x_bf = [tile([P, (hi - lo) * PACK], BF16, "x_bf%d" % c) for c, (lo, hi) in enumerate(FIRST)]
+        x_bf = [None] * len(FIRST)
         x_w = [tile([P, hi - lo], U32, "x_w%d" % c) for c, (lo, hi) in enumerate(FIRST)]
         x_s = [tile([P, hi - lo], U8, "x_s%d" % c) for c, (lo, hi) in enumerate(FIRST)]
         h_bf = [tile([P, (hi - lo) * PACK], BF16, "h_bf%d" % c) for c, (lo, hi) in enumerate(SECOND)]
@@ -188,14 +181,17 @@ def tile_list_htabg_mul_bias_kernel(tc, tab_words, tab_scales, xT, wgt2, wa, wb_
 
         def interleave_x(c):
             lo, hi = FIRST[c]
+            x_bf[c] = tile([P, (hi - lo) * PACK], BF16, "x_bf%d" % c, ("x_bf0", "wa_bf0", "slot_c", "wa_bf1")[c])
             nc.scalar.copy(
                 out=x_bf[c][:].rearrange("p (c i t) -> p c t i", t=PACK, i=4),
                 in_=picked[:].rearrange("p (t c i) -> p c t i", t=PACK, i=4)[:, lo // 4 : hi // 4],
             )
 
+        def quantize_x(c):
+            nc.vector.quantize_mx(out=x_w[c][:].bitcast(FP8X4), scales=x_s[c][:], in_=x_bf[c][:])
+
         def first_layer(c):
             lo, hi = FIRST[c]
-            nc.vector.quantize_mx(out=x_w[c][:].bitcast(FP8X4), scales=x_s[c][:], in_=x_bf[c][:])
             for s in range(lo // SUB, hi // SUB):
                 cols = slice(s * SUB - lo, (s + 1) * SUB - lo)
                 ya[s] = psum.tile([P, PACK, SUB], F32, name="bank")
@@ -256,14 +252,25 @@ def tile_list_htabg_mul_bias_kernel(tc, tab_words, tab_scales, xT, wgt2, wa, wb_
             queue.dma_start(out=out_rows[:, slices, lo:hi], in_=result[c][:, slices, :])
 
         last = len(SECOND) - 1
-        for c in range(len(FIRST)):
-            interleave_x(c)
+        interleave_x(0)
+        quantize_x(0)
+        interleave_wa(nc.vector.tensor_copy, 0)
+        interleave_wa(nc.scalar.copy, 1)
+        wa_s = tile([P, R], U8, "wa_s")
+        wa_w = tile([P, R], U32, "wa_w")
+        for h in range(2):
+            cols = slice(h * R // 2, (h + 1) * R // 2)
+            nc.vector.quantize_mx(out=wa_w[:, cols].bitcast(FP8X4), scales=wa_s[:, cols], in_=wa_bf[h][:])
         first_layer(0)
+        for c in range(1, len(FIRST)):
+            interleave_x(c)
+        quantize_x(1)
         first_layer(1)
         for s in range(J // SUB):
             product(s)
             for c, (lo, hi) in enumerate(FIRST[2:], 2):
                 if lo == (s + 3) * SUB:
+                    quantize_x(c)
                     first_layer(c)
             for c, (lo, hi) in enumerate(SECOND):
                 if hi == s * SUB:

@@ -23,6 +23,7 @@ SUB = 128
 STAGE = 112
 HEADS = 8
 RUN = J // P
+STORE = 256
 PARTS = [(0, 256), (256, 512), (512, 1024)]
 FIRST = [(0, 256), (256, 512), (512, 768), (768, 1024)]
 SECOND = [(0, 256), (256, 512), (512, 768), (768, 896), (896, 1024)]
@@ -106,7 +107,7 @@ def tile_list_htabg_mul_bias_kernel(tc, tab_words, tab_scales, xT, wgt2, wa, wb_
         )
         nc.vector.tensor_copy(both_rows[96:P, :J].bitcast(I32), v_rows[96:P, :].bitcast(I32))
         both_s = tile([P, J + R], U8, "both_s")
-        place_scale_rows(nc.sync, both_s, both_rows[STAGE:P, :])
+        place_scale_rows(nc.scalar, both_s, both_rows[STAGE:P, :])
         v_s = both_s[:, :J]
         wbp_s = both_s[:, J:]
 
@@ -138,8 +139,8 @@ def tile_list_htabg_mul_bias_kernel(tc, tab_words, tab_scales, xT, wgt2, wa, wb_
                     stop=True,
                 )
             nc.scalar.activation(
-                out=yb[s][:].rearrange("p (c t) -> p c t", t=PACK),
-                in_=acc[:].rearrange("p t c -> p c t"),
+                out=yb[s][:].rearrange("p (c t i) -> p c t i", t=PACK, i=4),
+                in_=acc[:].rearrange("p t (c i) -> p c t i", i=4),
                 func=IDENTITY,
             )
 
@@ -211,14 +212,18 @@ def tile_list_htabg_mul_bias_kernel(tc, tab_words, tab_scales, xT, wgt2, wa, wb_
             c = max(k for k, chunk in enumerate(SECOND) if chunk[0] <= s * SUB)
             first = (s * SUB - SECOND[c][0]) * PACK
             nc.vector.tensor_tensor(
-                h_bf[c][:, first : first + SUB * PACK].rearrange("p (c t) -> p c t", t=PACK),
-                ya[s][:].rearrange("p t c -> p c t"),
-                yb[s][:].rearrange("p (c t) -> p c t", t=PACK),
+                h_bf[c][:, first : first + SUB * PACK].rearrange("p (c i t) -> p c t i", t=PACK, i=4),
+                ya[s][:].rearrange("p t (c i) -> p c t i", i=4),
+                yb[s][:].rearrange("p (c t i) -> p c t i", t=PACK, i=4),
                 MULT,
             )
 
         y = {}
-        result = [tile([P, N // P, hi - lo], F32, "result%d" % c) for c, (lo, hi) in enumerate(SECOND)]
+        result = {(g, u): tile([P, 2, STORE], F32, "result%d_%d" % (g, u)) for g in range(J // STORE) for u in range(2)}
+
+        def place(c, u):
+            lo, hi = SECOND[c]
+            return result[lo // STORE, u][:, :, lo % STORE : lo % STORE + hi - lo]
 
         def second_layer(c):
             lo, hi = SECOND[c]
@@ -240,16 +245,15 @@ def tile_list_htabg_mul_bias_kernel(tc, tab_words, tab_scales, xT, wgt2, wa, wb_
         def empty_on_scalar(c, u):
             for v in range(2):
                 t = 2 * u + v
-                nc.scalar.activation(out=result[c][:, t, :], in_=y[c, u][:, v, :], func=IDENTITY, bias=bias[:, t : t + 1])
+                nc.scalar.activation(out=place(c, u)[:, v, :], in_=y[c, u][:, v, :], func=IDENTITY, bias=bias[:, t : t + 1])
 
         def empty_on_vector(c, u):
             lo, hi = SECOND[c]
             pair = slice(2 * u, 2 * u + 2)
-            nc.vector.tensor_tensor(result[c][:, pair, :], y[c, u][:], bias[:, pair].unsqueeze(2).to_broadcast([P, 2, hi - lo]), ADD)
+            nc.vector.tensor_tensor(place(c, u), y[c, u][:], bias[:, pair].unsqueeze(2).to_broadcast([P, 2, hi - lo]), ADD)
 
-        def store(queue, c, slices):
-            lo, hi = SECOND[c]
-            queue.dma_start(out=out_rows[:, slices, lo:hi], in_=result[c][:, slices, :])
+        def store(queue, g, u):
+            queue.dma_start(out=out_rows[:, 2 * u : 2 * u + 2, g * STORE : (g + 1) * STORE], in_=result[g, u][:])
 
         last = len(SECOND) - 1
         interleave_x(0)
@@ -273,17 +277,16 @@ def tile_list_htabg_mul_bias_kernel(tc, tab_words, tab_scales, xT, wgt2, wa, wb_
                     quantize_x(c)
                     first_layer(c)
             for c, (lo, hi) in enumerate(SECOND):
-                if hi == s * SUB:
+                if c < last and hi == (s + 1) * SUB:
                     second_layer(c)
                     empty_on_scalar(c, 0)
-                    store(nc.sync, c, slice(0, 2))
                     if c < last - 1:
+                        store(nc.sync, c, 0)
                         empty_on_scalar(c, 1)
-                        store(nc.sync, c, slice(2, 4))
+                        store(nc.sync, c, 1)
         second_layer(last)
         empty_on_scalar(last, 0)
+        store(nc.scalar, J // STORE - 1, 0)
         empty_on_vector(last - 1, 1)
-        store(nc.sync, last - 1, slice(2, 4))
-        store(nc.scalar, last, slice(0, 2))
         empty_on_vector(last, 1)
-        store(nc.sync, last, slice(2, 4))
+        store(nc.sync, J // STORE - 1, 1)

@@ -23,10 +23,9 @@ SUB = 128
 STAGE = 112
 HEADS = 8
 RUN = J // P
-STORE = 256
-PARTS = [(0, 256), (256, 512), (512, 1024)]
+PARTS = [(0, 256), (256, 1024)]
 FIRST = [(0, 256), (256, 512), (512, 768), (768, 1024)]
-SECOND = [(0, 256), (256, 512), (512, 768), (768, 896), (896, 1024)]
+SECOND = FIRST
 
 
 def place_scale_rows(queue, plane, rows):
@@ -139,8 +138,8 @@ def tile_list_htabg_mul_bias_kernel(tc, tab_words, tab_scales, xT, wgt2, wa, wb_
                     stop=True,
                 )
             nc.scalar.activation(
-                out=yb[s][:].rearrange("p (c t i) -> p c t i", t=PACK, i=4),
-                in_=acc[:].rearrange("p t (c i) -> p c t i", i=4),
+                out=yb[s][:].rearrange("p (c t) -> p c t", t=PACK),
+                in_=acc[:].rearrange("p t c -> p c t"),
                 func=IDENTITY,
             )
 
@@ -212,48 +211,40 @@ def tile_list_htabg_mul_bias_kernel(tc, tab_words, tab_scales, xT, wgt2, wa, wb_
             c = max(k for k, chunk in enumerate(SECOND) if chunk[0] <= s * SUB)
             first = (s * SUB - SECOND[c][0]) * PACK
             nc.vector.tensor_tensor(
-                h_bf[c][:, first : first + SUB * PACK].rearrange("p (c i t) -> p c t i", t=PACK, i=4),
-                ya[s][:].rearrange("p t (c i) -> p c t i", i=4),
-                yb[s][:].rearrange("p (c t i) -> p c t i", t=PACK, i=4),
+                h_bf[c][:, first : first + SUB * PACK].rearrange("p (c t) -> p c t", t=PACK),
+                ya[s][:].rearrange("p t c -> p c t"),
+                yb[s][:].rearrange("p (c t) -> p c t", t=PACK),
                 MULT,
             )
 
-        y = {}
-        result = {(g, u): tile([P, 2, STORE], F32, "result%d_%d" % (g, u)) for g in range(J // STORE) for u in range(2)}
-
-        def place(c, u):
-            lo, hi = SECOND[c]
-            return result[lo // STORE, u][:, :, lo % STORE : lo % STORE + hi - lo]
-
-        def second_layer(c):
-            lo, hi = SECOND[c]
+        def quantize_h(c):
             nc.vector.quantize_mx(out=h_w[c][:].bitcast(FP8X4), scales=h_s[c][:], in_=h_bf[c][:])
-            for u in range(2):
-                y[c, u] = psum.tile([P, 2, hi - lo], F32, name="bank")
-                for v in range(2):
-                    rows = slice((2 * u + v) * P, (2 * u + v + 1) * P)
-                    nc.tensor.matmul_mx(
-                        out=y[c, u][:, v, :],
-                        lhsT=wd_w[:, rows].bitcast(FP8X4),
-                        lhsT_scale=wd_s[:, rows],
-                        rhs=h_w[c][:].bitcast(FP8X4),
-                        rhs_scale=h_s[c][:],
-                        start=True,
-                        stop=True,
-                    )
 
-        def empty_on_scalar(c, u):
-            for v in range(2):
-                t = 2 * u + v
-                nc.scalar.activation(out=place(c, u)[:, v, :], in_=y[c, u][:, v, :], func=IDENTITY, bias=bias[:, t : t + 1])
-
-        def empty_on_vector(c, u):
+        def second_layer(c, slices):
             lo, hi = SECOND[c]
-            pair = slice(2 * u, 2 * u + 2)
-            nc.vector.tensor_tensor(place(c, u), y[c, u][:], bias[:, pair].unsqueeze(2).to_broadcast([P, 2, hi - lo]), ADD)
+            bank = psum.tile([P, len(slices), hi - lo], F32, name="bank")
+            for v, t in enumerate(slices):
+                rows = slice(t * P, (t + 1) * P)
+                nc.tensor.matmul_mx(
+                    out=bank[:, v, :],
+                    lhsT=wd_w[:, rows].bitcast(FP8X4),
+                    lhsT_scale=wd_s[:, rows],
+                    rhs=h_w[c][:].bitcast(FP8X4),
+                    rhs_scale=h_s[c][:],
+                    start=True,
+                    stop=True,
+                )
+            return bank
 
-        def store(queue, g, u):
-            queue.dma_start(out=out_rows[:, 2 * u : 2 * u + 2, g * STORE : (g + 1) * STORE], in_=result[g, u][:])
+        def empty_and_store(c, slices, bank, on_scalar, queue):
+            lo, hi = SECOND[c]
+            result = tile([P, len(slices), hi - lo], F32, "result%d_%d" % (c, slices[0]))
+            for v, t in enumerate(slices):
+                if on_scalar:
+                    nc.scalar.activation(out=result[:, v, :], in_=bank[:, v, :], func=IDENTITY, bias=bias[:, t : t + 1])
+                else:
+                    nc.vector.tensor_scalar(result[:, v, :], bank[:, v, :], bias[:, t : t + 1], None, ADD)
+            queue.dma_start(out=out_rows[:, slices[0] : slices[-1] + 1, lo:hi], in_=result[:])
 
         last = len(SECOND) - 1
         interleave_x(0)
@@ -278,15 +269,9 @@ def tile_list_htabg_mul_bias_kernel(tc, tab_words, tab_scales, xT, wgt2, wa, wb_
                     first_layer(c)
             for c, (lo, hi) in enumerate(SECOND):
                 if c < last and hi == (s + 1) * SUB:
-                    second_layer(c)
-                    empty_on_scalar(c, 0)
-                    if c < last - 1:
-                        store(nc.sync, c, 0)
-                        empty_on_scalar(c, 1)
-                        store(nc.sync, c, 1)
-        second_layer(last)
-        empty_on_scalar(last, 0)
-        store(nc.scalar, J // STORE - 1, 0)
-        empty_on_vector(last - 1, 1)
-        empty_on_vector(last, 1)
-        store(nc.sync, J // STORE - 1, 1)
+                    quantize_h(c)
+                    for slices in ((0, 1), (2, 3)):
+                        empty_and_store(c, slices, second_layer(c, slices), True, nc.sync)
+        quantize_h(last)
+        for t in range(N // P):
+            empty_and_store(last, (t,), second_layer(last, (t,)), t % 2 == 1, nc.scalar if t % 2 == 1 else nc.sync)

@@ -56,7 +56,7 @@ def tile_list_htabg_mul_bias_kernel(tc, tab_words, tab_scales, xT, wgt2, wa, wb_
         x_rows = xT.rearrange("(p i) t -> i p t", i=PACK)
         wa_rows = wa.rearrange("(p i) r -> p i r", i=PACK)
 
-        nc.vector.memset(tab_s[:STAGE, :].bitcast(I32), 0)
+        nc.gpsimd.memset(tab_s[:STAGE, :].bitcast(I32), 0)
         nc.gpsimd.memset(wb_s[:STAGE, :].bitcast(I32), 0)
 
         identity = tile([P, P], F32, "identity")
@@ -163,10 +163,10 @@ def tile_list_htabg_mul_bias_kernel(tc, tab_words, tab_scales, xT, wgt2, wa, wb_
         gather(2)
         wd_w = tile([P, N], I32, "wd_w", "slot_b")
         nc.sync.dma_start(out=wd_w[:], in_=words_of(wd_words))
-        bias = tile([P, N // P], F32, "bias", "slot_g")
+        gather(3)
+        bias = tile([P, N // P], F32, "bias", "wgt")
         with nc.allow_non_contiguous_dma(reason="one bias value a partition"):
             nc.sync.dma_start(out=bias[:], in_=b.rearrange("(t p) -> p t", p=P))
-        gather(3)
         wd_s = tile([P, N], U8, "wd_s", "slot_f")
         place_scale_rows(nc.sync, wd_s, wd_scales[0])
 

@@ -23,7 +23,7 @@ SUB = 128
 STAGE = 112
 HEADS = 8
 RUN = J // P
-PARTS = [(0, 256), (256, 1024)]
+PARTS = [(0, 256), (256, 768), (768, 1024)]
 FIRST = [(0, 256), (256, 512), (512, 768), (768, 1024)]
 SECOND = FIRST
 
@@ -62,11 +62,10 @@ def tile_list_htabg_mul_bias_kernel(tc, tab_words, tab_scales, xT, wgt2, wa, wb_
         identity = tile([P, P], F32, "identity")
         make_identity(nc, identity[:])
 
-        wa_bf = [tile([P, R * PACK // 2], BF16, "wa_bf%d" % h) for h in range(2)]
 
         def interleave_wa(copy, h):
             copy(
-                out=wa_bf[h][:].rearrange("p (t m i) -> p m i t", t=2, i=PACK),
+                out=wa_bf[h].rearrange("p (t m i) -> p m i t", t=2, i=PACK),
                 in_=wa_raw[:].rearrange("p i (m t) -> p m i t", t=PACK)[:, :, :, 2 * h : 2 * h + 2],
             )
 
@@ -143,10 +142,13 @@ def tile_list_htabg_mul_bias_kernel(tc, tab_words, tab_scales, xT, wgt2, wa, wb_
                 func=IDENTITY,
             )
 
-        picked = tile([P, PACK * J], F32, "picked")
+        late = PACK * J - 256
+        store = tile([P, late + R], F32, "picked")
+        picked = store[:, : PACK * J]
+        wa_bf = [tile([P, R * PACK // 2], BF16, "wa_bf0")[:], store[:, late:].bitcast(BF16)]
 
-        def gather(i):
-            for lo, hi in PARTS if i == PACK - 1 else [(0, J)]:
+        def gather(i, parts=((0, J),)):
+            for lo, hi in parts:
                 nc.vector.tensor_tensor(
                     picked[:, i * J + lo : i * J + hi],
                     x_plane[i][:].indirect(head_lists[:, lo // 16 : hi // 16]),
@@ -163,11 +165,11 @@ def tile_list_htabg_mul_bias_kernel(tc, tab_words, tab_scales, xT, wgt2, wa, wb_
         gather(2)
         wd_w = tile([P, N], I32, "wd_w", "slot_b")
         nc.sync.dma_start(out=wd_w[:], in_=words_of(wd_words))
-        gather(3)
-        bias = tile([P, N // P], F32, "bias", "wgt")
+        gather(3, PARTS[:2])
+        bias = tile([P, N // P], F32, "bias", "both_s")
         with nc.allow_non_contiguous_dma(reason="one bias value a partition"):
             nc.sync.dma_start(out=bias[:], in_=b.rearrange("(t p) -> p t", p=P))
-        wd_s = tile([P, N], U8, "wd_s", "slot_f")
+        wd_s = tile([P, N], U8, "wd_s", "wbp_w")
         place_scale_rows(nc.sync, wd_s, wd_scales[0])
 
         x_bf = [None] * len(FIRST)
@@ -181,10 +183,10 @@ def tile_list_htabg_mul_bias_kernel(tc, tab_words, tab_scales, xT, wgt2, wa, wb_
 
         def interleave_x(c):
             lo, hi = FIRST[c]
-            x_bf[c] = tile([P, (hi - lo) * PACK], BF16, "x_bf%d" % c, ("x_bf0", "wa_bf0", "slot_c", "wa_bf1")[c])
+            x_bf[c] = tile([P, (hi - lo) * PACK], BF16, "x_bf%d" % c, ("x_bf0", "x_bf1", "slot_c", "x_bf3")[c])
             nc.scalar.copy(
                 out=x_bf[c][:].rearrange("p (c i t) -> p c t i", t=PACK, i=4),
-                in_=picked[:].rearrange("p (t c i) -> p c t i", t=PACK, i=4)[:, lo // 4 : hi // 4],
+                in_=picked.rearrange("p (t c i) -> p c t i", t=PACK, i=4)[:, lo // 4 : hi // 4],
             )
 
         def quantize_x(c):
@@ -255,9 +257,11 @@ def tile_list_htabg_mul_bias_kernel(tc, tab_words, tab_scales, xT, wgt2, wa, wb_
         wa_w = tile([P, R], U32, "wa_w")
         for h in range(2):
             cols = slice(h * R // 2, (h + 1) * R // 2)
-            nc.vector.quantize_mx(out=wa_w[:, cols].bitcast(FP8X4), scales=wa_s[:, cols], in_=wa_bf[h][:])
+            nc.vector.quantize_mx(out=wa_w[:, cols].bitcast(FP8X4), scales=wa_s[:, cols], in_=wa_bf[h])
         first_layer(0)
-        for c in range(1, len(FIRST)):
+        interleave_x(1)
+        gather(3, PARTS[2:])
+        for c in range(2, len(FIRST)):
             interleave_x(c)
         quantize_x(1)
         first_layer(1)

@@ -73,10 +73,10 @@ def tile_list_htabg_mul_bias_kernel(tc, tab_words, tab_scales, xT, wgt2, wa, wb_
         nc.gpsimd.memset(head_w[HEADS * RUN :, :], 0.0)
         nc.sync.dma_start(tab_list[:], offs)
         nc.sync.dma_start(out=tab_s[STAGE:P, :].bitcast(I32), in_=tab_scales[0].bitcast(I32))
-        nc.sync.dma_start(out=wb_s[STAGE:P, :].bitcast(I32), in_=wb_scales[0].bitcast(I32))
-        nc.sync.dma_start(out=head_w[: HEADS * RUN, :], in_=wgt2.rearrange("(g s) (u v) -> s g u v", s=16, v=P)[0])
-        nc.sync.dma_start(head_lists[:], offs2)
+        nc.scalar.dma_start(out=wb_s[STAGE:P, :].bitcast(I32), in_=wb_scales[0].bitcast(I32))
+        nc.scalar.dma_start(out=head_w[: HEADS * RUN, :], in_=wgt2.rearrange("(g s) (u v) -> s g u v", s=16, v=P)[0])
         nc.sync.dma_start(out=tab_w[:], in_=words_of(tab_words))
+        nc.sync.dma_start(head_lists[:], offs2)
         nc.sync.dma_start(out=wb_w[:], in_=words_of(wb_words))
         x_plane = [tile([P, T], F32, "x_plane0", "slot_e")]
         nc.sync.dma_start(out=x_plane[0][:], in_=x_rows[0])
@@ -238,6 +238,28 @@ def tile_list_htabg_mul_bias_kernel(tc, tab_words, tab_scales, xT, wgt2, wa, wb_
                 )
             return bank
 
+        def second_layer_by_halves(c, slices_a_bank):
+            banks = [psum.tile([P, slices_a_bank, 2 * SUB], F32, name="bank") for first in range(0, N // P, slices_a_bank)]
+            for half in range(2):
+                cols = slice(half * SUB, (half + 1) * SUB)
+                nc.vector.quantize_mx(
+                    out=h_w[c][:, cols].bitcast(FP8X4),
+                    scales=h_s[c][:, cols],
+                    in_=h_bf[c][:, half * SUB * PACK : (half + 1) * SUB * PACK],
+                )
+                for t in range(N // P):
+                    rows = slice(t * P, (t + 1) * P)
+                    nc.tensor.matmul_mx(
+                        out=banks[t // slices_a_bank][:, t % slices_a_bank, cols],
+                        lhsT=wd_w[:, rows].bitcast(FP8X4),
+                        lhsT_scale=wd_s[:, rows],
+                        rhs=h_w[c][:, cols].bitcast(FP8X4),
+                        rhs_scale=h_s[c][:, cols],
+                        start=True,
+                        stop=True,
+                    )
+            return [banks[t // slices_a_bank][:, t % slices_a_bank : t % slices_a_bank + 1, :] for t in range(N // P)]
+
         def empty_and_store(c, slices, bank, on_scalar, queue):
             lo, hi = SECOND[c]
             result = tile([P, len(slices), hi - lo], F32, "result%d_%d" % (c, slices[0]))
@@ -272,10 +294,12 @@ def tile_list_htabg_mul_bias_kernel(tc, tab_words, tab_scales, xT, wgt2, wa, wb_
                     quantize_x(c)
                     first_layer(c)
             for c, (lo, hi) in enumerate(SECOND):
-                if c < last and hi == (s + 1) * SUB:
+                if c < last - 1 and hi == (s + 1) * SUB:
                     quantize_h(c)
                     for slices in ((0, 1), (2, 3)):
                         empty_and_store(c, slices, second_layer(c, slices), True, nc.sync)
-        quantize_h(last)
-        for t in range(N // P):
-            empty_and_store(last, (t,), second_layer(last, (t,)), t % 2 == 1, nc.scalar if t % 2 == 1 else nc.sync)
+                if c == last - 1 and hi == (s + 1) * SUB:
+                    for t, bank in enumerate(second_layer_by_halves(c, 2)):
+                        empty_and_store(c, (t,), bank, True, nc.sync)
+        for t, bank in enumerate(second_layer_by_halves(last, 1)):
+            empty_and_store(last, (t,), bank, t % 2 == 1, nc.scalar if t % 2 == 1 else nc.sync)

@@ -41,10 +41,14 @@ def tile_list_htabg_mul_bias_kernel(tc, tab_words, tab_scales, xT, wgt2, wa, wb_
     nc = tc.nc
     with ExitStack() as ctx:
         keep = ctx.enter_context(tc.tile_pool(name="keep", bufs=1))
-        psum = ctx.enter_context(tc.psum_pool(name="psum", bufs=8))
+        late = ctx.enter_context(tc.tile_pool(name="late", bufs=1))
+        psum = ctx.enter_context(tc.psum_pool(name="psum", bufs=1))
 
         def tile(shape, dtype, name, slot=""):
             return keep.tile(shape, dtype, name=name, tag=slot or name, align_bytes=64)
+
+        def bank_tile(shape, number):
+            return psum.tile(shape, F32, name="bank%d" % number)
 
         tab_list = keep.tile([P, J // 16], U16, name="tab_list")
         head_lists = keep.tile([P, J // 16], U16, name="head_lists")
@@ -74,7 +78,7 @@ def tile_list_htabg_mul_bias_kernel(tc, tab_words, tab_scales, xT, wgt2, wa, wb_
         nc.sync.dma_start(tab_list[:], offs)
         nc.sync.dma_start(out=tab_s[STAGE:P, :].bitcast(I32), in_=tab_scales[0].bitcast(I32))
         nc.scalar.dma_start(out=wb_s[STAGE:P, :].bitcast(I32), in_=wb_scales[0].bitcast(I32))
-        nc.scalar.dma_start(out=head_w[: HEADS * RUN, :], in_=wgt2.rearrange("(g s) (u v) -> s g u v", s=16, v=P)[0])
+        nc.scalar.dma_start(out=head_w[: HEADS * RUN, :], in_=wgt2.rearrange("p (h v) -> (p h) v", h=2)[::17].rearrange("a (u v) -> a u v", v=P))
         nc.sync.dma_start(out=tab_w[:], in_=words_of(tab_words))
         nc.sync.dma_start(head_lists[:], offs2)
         nc.sync.dma_start(out=wb_w[:], in_=words_of(wb_words))
@@ -84,21 +88,21 @@ def tile_list_htabg_mul_bias_kernel(tc, tab_words, tab_scales, xT, wgt2, wa, wb_
         nc.sync.dma_start(out=x_plane[1][:], in_=x_rows[1])
 
         spread = tile([P, RUN, P], F32, "spread")
-        by_token = psum.tile([P, P], F32, name="bank")
+        by_token = bank_tile([P, P], 5)
         nc.tensor.transpose(by_token[:], head_w[:], identity[:])
         nc.scalar.copy(
             out=spread[:].rearrange("v u (g s) -> v u g s", s=16),
             in_=by_token[:, : HEADS * RUN].rearrange("v (g u) -> v u g", u=RUN).unsqueeze(3).to_broadcast([P, RUN, HEADS, 16]),
         )
         for u in range(RUN // PACK):
-            turned = psum.tile([P, PACK, SUB], F32, name="bank")
+            turned = bank_tile([P, PACK, SUB], 6 + u)
             for c in range(PACK):
                 nc.tensor.transpose(turned[:, c, :], spread[:, PACK * u + c, :], identity[:])
             nc.scalar.copy(out=wgt[:, u * PACK * P : (u + 1) * PACK * P], in_=turned[:].rearrange("p c v -> p (c v)"))
 
         v_rows = tile([P, J], U8, "v_rows")
         nc.vector.tensor_copy(v_rows[:], tab_s[:].indirect(tab_list[:]))
-        both_rows = tile([P, J + R], U8, "both_rows", "slot_c")
+        both_rows = late.tile([P, J + R], U8, name="both_rows", offset=0, align_bytes=64)
         nc.gpsimd.tensor_copy(
             out=both_rows[:, J:].rearrange("p (t c i) -> p c t i", t=PACK, i=16),
             in_=wb_s[:].rearrange("p (c i t) -> p c t i", t=PACK, i=16),
@@ -121,10 +125,11 @@ def tile_list_htabg_mul_bias_kernel(tc, tab_words, tab_scales, xT, wgt2, wa, wb_
         )
 
 
-        yb = [tile([P, SUB * PACK], F32, "yb%d" % s) for s in range(J // SUB)]
-        for s in range(J // SUB):
+        yb = {}
+
+        def table_layer(s):
             cols = slice(s * SUB, (s + 1) * SUB)
-            acc = psum.tile([P, PACK, SUB], F32, name="bank")
+            acc = bank_tile([P, PACK, SUB], s)
             for t in range(PACK):
                 rows = slice(t * P, (t + 1) * P)
                 nc.tensor.matmul_mx(
@@ -136,16 +141,24 @@ def tile_list_htabg_mul_bias_kernel(tc, tab_words, tab_scales, xT, wgt2, wa, wb_
                     start=True,
                     stop=True,
                 )
+            return acc
+
+        def copy_yb(s, acc, yb_s):
+            yb[s] = yb_s
             nc.scalar.activation(
                 out=yb[s][:].rearrange("p (c t) -> p c t", t=PACK),
                 in_=acc[:].rearrange("p t c -> p c t"),
                 func=IDENTITY,
             )
 
-        late = PACK * J - 256
-        store = tile([P, late + R], F32, "picked")
+        for s in range(J // SUB - 1):
+            copy_yb(s, table_layer(s), tile([P, SUB * PACK], F32, "yb%d" % s))
+        yb_bank = table_layer(J // SUB - 1)
+
+        tail = PACK * J - 256
+        store = tile([P, tail + R], F32, "picked")
         picked = store[:, : PACK * J]
-        wa_bf = [tile([P, R * PACK // 2], BF16, "wa_bf0")[:], store[:, late:].bitcast(BF16)]
+        wa_bf = [tile([P, R * PACK // 2], BF16, "wa_bf0")[:], store[:, tail:].bitcast(BF16)]
 
         def gather(i, parts=((0, J),)):
             for lo, hi in parts:
@@ -158,7 +171,7 @@ def tile_list_htabg_mul_bias_kernel(tc, tab_words, tab_scales, xT, wgt2, wa, wb_
 
         x_plane.append(tile([P, T], F32, "x_plane3", "slot_f"))
         nc.sync.dma_start(out=x_plane[3][:], in_=x_rows[3])
-        wa_raw = tile([P, PACK, R], F32, "wa_raw", "slot_c")
+        wa_raw = late.tile([P, PACK, R], F32, name="wa_raw", offset=0, align_bytes=64)
         nc.sync.dma_start(out=wa_raw[:], in_=wa_rows)
         gather(0)
         gather(1)
@@ -183,7 +196,10 @@ def tile_list_htabg_mul_bias_kernel(tc, tab_words, tab_scales, xT, wgt2, wa, wb_
 
         def interleave_x(c):
             lo, hi = FIRST[c]
-            x_bf[c] = tile([P, (hi - lo) * PACK], BF16, "x_bf%d" % c, ("x_bf0", "x_bf1", "slot_c", "x_bf3")[c])
+            if c == 2:
+                x_bf[c] = late.tile([P, (hi - lo) * PACK], BF16, name="x_bf2", offset=0, align_bytes=64)
+            else:
+                x_bf[c] = tile([P, (hi - lo) * PACK], BF16, "x_bf%d" % c)
             nc.scalar.copy(
                 out=x_bf[c][:].rearrange("p (c i t) -> p c t i", t=PACK, i=4),
                 in_=picked.rearrange("p (t c i) -> p c t i", t=PACK, i=4)[:, lo // 4 : hi // 4],
@@ -196,7 +212,7 @@ def tile_list_htabg_mul_bias_kernel(tc, tab_words, tab_scales, xT, wgt2, wa, wb_
             lo, hi = FIRST[c]
             for s in range(lo // SUB, hi // SUB):
                 cols = slice(s * SUB - lo, (s + 1) * SUB - lo)
-                ya[s] = psum.tile([P, PACK, SUB], F32, name="bank")
+                ya[s] = bank_tile([P, PACK, SUB], 1 + (s - 1) % 3 if s else 0)
                 for t in range(PACK):
                     rows = slice(t * P, (t + 1) * P)
                     nc.tensor.matmul_mx(
@@ -224,7 +240,7 @@ def tile_list_htabg_mul_bias_kernel(tc, tab_words, tab_scales, xT, wgt2, wa, wb_
 
         def second_layer(c, slices):
             lo, hi = SECOND[c]
-            bank = psum.tile([P, len(slices), hi - lo], F32, name="bank")
+            bank = bank_tile([P, len(slices), hi - lo], 4 + 2 * c + slices[0] // 2)
             for v, t in enumerate(slices):
                 rows = slice(t * P, (t + 1) * P)
                 nc.tensor.matmul_mx(
@@ -238,8 +254,9 @@ def tile_list_htabg_mul_bias_kernel(tc, tab_words, tab_scales, xT, wgt2, wa, wb_
                 )
             return bank
 
-        def second_layer_by_halves(c, slices_a_bank):
-            banks = [psum.tile([P, slices_a_bank, 2 * SUB], F32, name="bank") for first in range(0, N // P, slices_a_bank)]
+        def second_layer_by_halves(c, numbers):
+            slices_a_bank = N // P // len(numbers)
+            banks = [bank_tile([P, slices_a_bank, 2 * SUB], number) for number in numbers]
             for half in range(2):
                 cols = slice(half * SUB, (half + 1) * SUB)
                 nc.vector.quantize_mx(
@@ -285,6 +302,7 @@ def tile_list_htabg_mul_bias_kernel(tc, tab_words, tab_scales, xT, wgt2, wa, wb_
         gather(3, PARTS[2:])
         for c in range(2, len(FIRST)):
             interleave_x(c)
+        copy_yb(J // SUB - 1, yb_bank, late.tile([P, SUB * PACK], F32, name="yb_last", offset=2048, align_bytes=64))
         quantize_x(1)
         first_layer(1)
         for s in range(J // SUB):
@@ -299,7 +317,7 @@ def tile_list_htabg_mul_bias_kernel(tc, tab_words, tab_scales, xT, wgt2, wa, wb_
                     for slices in ((0, 1), (2, 3)):
                         empty_and_store(c, slices, second_layer(c, slices), True, nc.sync)
                 if c == last - 1 and hi == (s + 1) * SUB:
-                    for t, bank in enumerate(second_layer_by_halves(c, 2)):
+                    for t, bank in enumerate(second_layer_by_halves(c, (0, 2))):
                         empty_and_store(c, (t,), bank, True, nc.sync)
-        for t, bank in enumerate(second_layer_by_halves(last, 1)):
+        for t, bank in enumerate(second_layer_by_halves(last, (4, 5, 6, 7))):
             empty_and_store(last, (t,), bank, t % 2 == 1, nc.scalar if t % 2 == 1 else nc.sync)

@@ -76,10 +76,10 @@ def tile_list_htabg_mul_bias_kernel(tc, tab_words, tab_scales, xT, wgt2, wa, wb_
         head_w = tile([P, P], F32, "head_w")
         nc.gpsimd.memset(head_w[HEADS * RUN :, :], 0.0)
         nc.sync.dma_start(tab_list[:], offs)
-        nc.sync.dma_start(out=tab_s[STAGE:P, :].bitcast(I32), in_=tab_scales[0].bitcast(I32))
-        nc.scalar.dma_start(out=wb_s[STAGE:P, :].bitcast(I32), in_=wb_scales[0].bitcast(I32))
-        nc.scalar.dma_start(out=head_w[: HEADS * RUN, :], in_=wgt2.rearrange("p (h v) -> (p h) v", h=2)[::17].rearrange("a (u v) -> a u v", v=P))
+        nc.scalar.dma_start(out=tab_s[STAGE:P, :].bitcast(I32), in_=tab_scales[0].bitcast(I32))
+        nc.sync.dma_start(out=head_w[: HEADS * RUN, :], in_=wgt2.rearrange("p (h v) -> (p h) v", h=2)[::17].rearrange("a (u v) -> a u v", v=P))
         nc.sync.dma_start(out=tab_w[:], in_=words_of(tab_words))
+        nc.sync.dma_start(out=wb_s[STAGE:P, :].bitcast(I32), in_=wb_scales[0].bitcast(I32))
         nc.sync.dma_start(head_lists[:], offs2)
         nc.sync.dma_start(out=wb_w[:], in_=words_of(wb_words))
         x_plane = [tile([P, T], F32, "x_plane0", "slot_e")]
@@ -103,11 +103,11 @@ def tile_list_htabg_mul_bias_kernel(tc, tab_words, tab_scales, xT, wgt2, wa, wb_
         v_rows = tile([P, J], U8, "v_rows")
         nc.vector.tensor_copy(v_rows[:], tab_s[:].indirect(tab_list[:]))
         both_rows = late.tile([P, J + R], U8, name="both_rows", offset=0, align_bytes=64)
+        nc.vector.tensor_copy(both_rows[96:P, :J].bitcast(I32), v_rows[96:P, :].bitcast(I32))
         nc.gpsimd.tensor_copy(
             out=both_rows[:, J:].rearrange("p (t c i) -> p c t i", t=PACK, i=16),
             in_=wb_s[:].rearrange("p (c i t) -> p c t i", t=PACK, i=16),
         )
-        nc.vector.tensor_copy(both_rows[96:P, :J].bitcast(I32), v_rows[96:P, :].bitcast(I32))
         both_s = tile([P, J + R], U8, "both_s")
         place_scale_rows(nc.scalar, both_s, both_rows[STAGE:P, :])
         v_s = both_s[:, :J]
@@ -320,4 +320,4 @@ def tile_list_htabg_mul_bias_kernel(tc, tab_words, tab_scales, xT, wgt2, wa, wb_
                     for t, bank in enumerate(second_layer_by_halves(c, (0, 2))):
                         empty_and_store(c, (t,), bank, True, nc.sync)
         for t, bank in enumerate(second_layer_by_halves(last, (4, 5, 6, 7))):
-            empty_and_store(last, (t,), bank, t % 2 == 1, nc.scalar if t % 2 == 1 else nc.sync)
+            empty_and_store(last, (t,), bank, t % 2 == 1, nc.scalar if t == N // P - 1 else nc.sync)

@@ -315,7 +315,9 @@ def tile_list_htabg_mul_bias_kernel(tc, tab_words, tab_scales, xT, wgt2, wa, wb_
                 if c < last - 1 and hi == (s + 1) * SUB:
                     quantize_h(c)
                     for slices in ((0, 1), (2, 3)):
-                        empty_and_store(c, slices, second_layer(c, slices), True, nc.sync)
+                        bank = second_layer(c, slices)
+                        for v, t in enumerate(slices):
+                            empty_and_store(c, (t,), bank[:, v : v + 1, :], True, nc.sync)
                 if c == last - 1 and hi == (s + 1) * SUB:
                     for t, bank in enumerate(second_layer_by_halves(c, (0, 2))):
                         empty_and_store(c, (t,), bank, True, nc.sync)

@@ -20,12 +20,18 @@ IDENTITY = mybir.ActivationFunctionType.Identity
 P = 128
 PACK = 4
 SUB = 128
+CHUNK = 256
 STAGE = 112
 HEADS = 8
 RUN = J // P
-PARTS = [(0, 256), (256, 768), (768, 1024)]
-FIRST = [(0, 256), (256, 512), (512, 768), (768, 1024)]
-SECOND = FIRST
+KIB = 1024
+CHUNKS = J // CHUNK
+EARLY = 2
+RING = 4
+SHARE = 48
+H_KIB = (38, 42, 43, 44, 39)
+YA_BANKS = (0, 1, 2, 3, 0, 3, 2, 1)
+OUT_BANKS = ((4, 5), (6, 7), (4, 5), (6, 7, 0, 3))
 
 
 def place_scale_rows(queue, plane, rows):
@@ -41,51 +47,54 @@ def tile_list_htabg_mul_bias_kernel(tc, tab_words, tab_scales, xT, wgt2, wa, wb_
     nc = tc.nc
     with ExitStack() as ctx:
         keep = ctx.enter_context(tc.tile_pool(name="keep", bufs=1))
-        late = ctx.enter_context(tc.tile_pool(name="late", bufs=1))
+        laid = ctx.enter_context(tc.tile_pool(name="laid", bufs=1))
         psum = ctx.enter_context(tc.psum_pool(name="psum", bufs=1))
 
         def tile(shape, dtype, name, slot=""):
             return keep.tile(shape, dtype, name=name, tag=slot or name, align_bytes=64)
 
+        def tile_at(kib, shape, dtype, name):
+            return laid.tile(shape, dtype, name=name, offset=kib * KIB, align_bytes=64)
+
         def bank_tile(shape, number):
             return psum.tile(shape, F32, name="bank%d" % number)
 
+        def mx(out_ap, w_words, w_scales, a_words, a_scales):
+            nc.tensor.matmul_mx(
+                out=out_ap,
+                lhsT=w_words.bitcast(FP8X4),
+                lhsT_scale=w_scales,
+                rhs=a_words.bitcast(FP8X4),
+                rhs_scale=a_scales,
+                start=True,
+                stop=True,
+            )
+
         tab_list = keep.tile([P, J // 16], U16, name="tab_list")
         head_lists = keep.tile([P, J // 16], U16, name="head_lists")
-        tab_s = tile([P, T], U8, "tab_s", "slot_a")
-        tab_w = tile([P, T], I32, "tab_w", "slot_b")
-        wb_w = tile([P, R], I32, "wb_w", "slot_f")
-        wb_s = tile([P, R], U8, "wb_s")
+        tab_s = tile([P, T], U8, "tab_s")
+        tab_w = tile([P, T], I32, "tab_w", "slot_tab")
+        wb_w = tile([P, R], I32, "wb_w", "slot_wb")
+        wb_s = tile_at(24, [P, R], U8, "wb_s")
         wgt = tile([P, J], F32, "wgt")
+        head_w = tile([P, P], F32, "head_w")
+        identity = tile([P, P], F32, "identity")
         x_rows = xT.rearrange("(p i) t -> i p t", i=PACK)
-        wa_rows = wa.rearrange("(p i) r -> p i r", i=PACK)
 
         nc.gpsimd.memset(tab_s[:STAGE, :].bitcast(I32), 0)
         nc.gpsimd.memset(wb_s[:STAGE, :].bitcast(I32), 0)
-
-        identity = tile([P, P], F32, "identity")
         make_identity(nc, identity[:])
-
-
-        def interleave_wa(copy, h):
-            copy(
-                out=wa_bf[h].rearrange("p (t m i) -> p m i t", t=2, i=PACK),
-                in_=wa_raw[:].rearrange("p i (m t) -> p m i t", t=PACK)[:, :, :, 2 * h : 2 * h + 2],
-            )
-
-        head_w = tile([P, P], F32, "head_w")
         nc.gpsimd.memset(head_w[HEADS * RUN :, :], 0.0)
+
         nc.sync.dma_start(tab_list[:], offs)
         nc.scalar.dma_start(out=tab_s[STAGE:P, :].bitcast(I32), in_=tab_scales[0].bitcast(I32))
         nc.sync.dma_start(out=head_w[: HEADS * RUN, :], in_=wgt2.rearrange("p (h v) -> (p h) v", h=2)[::17].rearrange("a (u v) -> a u v", v=P))
+        nc.scalar.dma_start(out=wb_s[STAGE:P, :].bitcast(I32), in_=wb_scales[0].bitcast(I32))
         nc.sync.dma_start(out=tab_w[:], in_=words_of(tab_words))
-        nc.sync.dma_start(out=wb_s[STAGE:P, :].bitcast(I32), in_=wb_scales[0].bitcast(I32))
         nc.sync.dma_start(head_lists[:], offs2)
         nc.sync.dma_start(out=wb_w[:], in_=words_of(wb_words))
-        x_plane = [tile([P, T], F32, "x_plane0", "slot_e")]
+        x_plane = [tile_at(4, [P, T], F32, "x_plane0")]
         nc.sync.dma_start(out=x_plane[0][:], in_=x_rows[0])
-        x_plane.append(tile([P, T], F32, "x_plane1", "slot_g"))
-        nc.sync.dma_start(out=x_plane[1][:], in_=x_rows[1])
 
         spread = tile([P, RUN, P], F32, "spread")
         by_token = bank_tile([P, P], 5)
@@ -100,22 +109,24 @@ def tile_list_htabg_mul_bias_kernel(tc, tab_words, tab_scales, xT, wgt2, wa, wb_
                 nc.tensor.transpose(turned[:, c, :], spread[:, PACK * u + c, :], identity[:])
             nc.scalar.copy(out=wgt[:, u * PACK * P : (u + 1) * PACK * P], in_=turned[:].rearrange("p c v -> p (c v)"))
 
-        v_rows = tile([P, J], U8, "v_rows")
+        v_rows = tile_at(25, [P, J], U8, "v_rows")
         nc.vector.tensor_copy(v_rows[:], tab_s[:].indirect(tab_list[:]))
-        both_rows = late.tile([P, J + R], U8, name="both_rows", offset=0, align_bytes=64)
+        both_rows = tile_at(26, [P, J + R], U8, "both_rows")
         nc.vector.tensor_copy(both_rows[96:P, :J].bitcast(I32), v_rows[96:P, :].bitcast(I32))
         nc.gpsimd.tensor_copy(
             out=both_rows[:, J:].rearrange("p (t c i) -> p c t i", t=PACK, i=16),
             in_=wb_s[:].rearrange("p (c i t) -> p c t i", t=PACK, i=16),
         )
         both_s = tile([P, J + R], U8, "both_s")
-        place_scale_rows(nc.scalar, both_s, both_rows[STAGE:P, :])
+        place_scale_rows(nc.sync, both_s, both_rows[STAGE:P, :])
         v_s = both_s[:, :J]
         wbp_s = both_s[:, J:]
+        x_plane.append(tile_at(18, [P, T], F32, "x_plane1"))
+        nc.sync.dma_start(out=x_plane[1][:], in_=x_rows[1])
 
-        v_w = tile([P, J], U32, "v_w")
+        v_w = tile_at(37, [P, J], U32, "v_w")
         nc.vector.tensor_copy(v_w[:], tab_w[:].bitcast(U32).indirect(tab_list[:]))
-        x_plane.append(tile([P, T], F32, "x_plane2", "slot_b"))
+        x_plane.append(tile_at(27, [P, T], F32, "x_plane2"))
         nc.sync.dma_start(out=x_plane[2][:], in_=x_rows[2])
 
         wbp_w = tile([P, R], I32, "wbp_w")
@@ -124,202 +135,152 @@ def tile_list_htabg_mul_bias_kernel(tc, tab_words, tab_scales, xT, wgt2, wa, wb_
             in_=wb_w[:].rearrange("p (c i t) -> p c t i", t=PACK, i=4),
         )
 
-
-        yb = {}
-
-        def table_layer(s):
-            cols = slice(s * SUB, (s + 1) * SUB)
-            acc = bank_tile([P, PACK, SUB], s)
+        def first_layer(number, w_words, w_scales, a_words, a_scales):
+            acc = bank_tile([P, PACK, SUB], number)
             for t in range(PACK):
                 rows = slice(t * P, (t + 1) * P)
-                nc.tensor.matmul_mx(
-                    out=acc[:, t, :],
-                    lhsT=wbp_w[:, rows].bitcast(FP8X4),
-                    lhsT_scale=wbp_s[:, rows],
-                    rhs=v_w[:, cols].bitcast(FP8X4),
-                    rhs_scale=v_s[:, cols],
-                    start=True,
-                    stop=True,
-                )
+                mx(acc[:, t, :], w_words[:, rows], w_scales[:, rows], a_words, a_scales)
             return acc
 
-        def copy_yb(s, acc, yb_s):
-            yb[s] = yb_s
-            nc.scalar.activation(
-                out=yb[s][:].rearrange("p (c t) -> p c t", t=PACK),
-                in_=acc[:].rearrange("p t c -> p c t"),
-                func=IDENTITY,
+        yb = []
+        for s in range(J // SUB):
+            cols = slice(s * SUB, (s + 1) * SUB)
+            acc = first_layer(s % RING, wbp_w, wbp_s, v_w[:, cols], v_s[:, cols])
+            yb.append(tile([P, SUB, PACK], F32, "yb%d" % s))
+            nc.scalar.activation(out=yb[s][:], in_=acc[:].rearrange("p t c -> p c t"), func=IDENTITY)
+
+        picked = tile([P, PACK * J], F32, "picked")[:]
+        wa_bf = [
+            tile([P, 2, R], BF16, "wa_bf0")[:],
+            picked[:, 3 * J :].bitcast(BF16).rearrange("p (c w) -> p c w", c=CHUNKS)[:, 0 : CHUNKS : CHUNKS - 1],
+        ]
+
+        def gather(i, lo, hi):
+            nc.vector.tensor_tensor(
+                picked[:, i * J + lo : i * J + hi],
+                x_plane[i][:].indirect(head_lists[:, lo // 16 : hi // 16]),
+                wgt[:, lo:hi],
+                MULT,
             )
 
-        for s in range(J // SUB - 1):
-            copy_yb(s, table_layer(s), tile([P, SUB * PACK], F32, "yb%d" % s))
-        yb_bank = table_layer(J // SUB - 1)
+        x_bf = {}
+        x_w = [tile_at(10, [P, CHUNK], U32, "x_w1") if c == 1 else tile([P, CHUNK], U32, "x_w%d" % c) for c in range(CHUNKS)]
+        x_s = [tile([P, CHUNK], U8, "x_s%d" % c) for c in range(CHUNKS)]
 
-        tail = PACK * J - 256
-        store = tile([P, tail + R], F32, "picked")
-        picked = store[:, : PACK * J]
-        wa_bf = [tile([P, R * PACK // 2], BF16, "wa_bf0")[:], store[:, tail:].bitcast(BF16)]
-
-        def gather(i, parts=((0, J),)):
-            for lo, hi in parts:
-                nc.vector.tensor_tensor(
-                    picked[:, i * J + lo : i * J + hi],
-                    x_plane[i][:].indirect(head_lists[:, lo // 16 : hi // 16]),
-                    wgt[:, lo:hi],
-                    MULT,
-                )
-
-        x_plane.append(tile([P, T], F32, "x_plane3", "slot_f"))
-        nc.sync.dma_start(out=x_plane[3][:], in_=x_rows[3])
-        wa_raw = late.tile([P, PACK, R], F32, name="wa_raw", offset=0, align_bytes=64)
-        nc.sync.dma_start(out=wa_raw[:], in_=wa_rows)
-        gather(0)
-        gather(1)
-        gather(2)
-        wd_w = tile([P, N], I32, "wd_w", "slot_b")
-        nc.sync.dma_start(out=wd_w[:], in_=words_of(wd_words))
-        gather(3, PARTS[:2])
-        bias = tile([P, N // P], F32, "bias", "both_s")
-        with nc.allow_non_contiguous_dma(reason="one bias value a partition"):
-            nc.sync.dma_start(out=bias[:], in_=b.rearrange("(t p) -> p t", p=P))
-        wd_s = tile([P, N], U8, "wd_s", "wbp_w")
-        place_scale_rows(nc.sync, wd_s, wd_scales[0])
-
-        x_bf = [None] * len(FIRST)
-        x_w = [tile([P, hi - lo], U32, "x_w%d" % c) for c, (lo, hi) in enumerate(FIRST)]
-        x_s = [tile([P, hi - lo], U8, "x_s%d" % c) for c, (lo, hi) in enumerate(FIRST)]
-        h_bf = [tile([P, (hi - lo) * PACK], BF16, "h_bf%d" % c) for c, (lo, hi) in enumerate(SECOND)]
-        h_w = [tile([P, hi - lo], U32, "h_w%d" % c) for c, (lo, hi) in enumerate(SECOND)]
-        h_s = [tile([P, hi - lo], U8, "h_s%d" % c) for c, (lo, hi) in enumerate(SECOND)]
-        out_rows = out.rearrange("(t p) j -> p t j", p=P)
-        ya = {}
-
-        def interleave_x(c):
-            lo, hi = FIRST[c]
-            if c == 2:
-                x_bf[c] = late.tile([P, (hi - lo) * PACK], BF16, name="x_bf2", offset=0, align_bytes=64)
-            else:
-                x_bf[c] = tile([P, (hi - lo) * PACK], BF16, "x_bf%d" % c)
+        def weave_x(c, first, count):
+            tokens = slice(c * CHUNK // 4, (c + 1) * CHUNK // 4)
             nc.scalar.copy(
-                out=x_bf[c][:].rearrange("p (c i t) -> p c t i", t=PACK, i=4),
-                in_=picked.rearrange("p (t c i) -> p c t i", t=PACK, i=4)[:, lo // 4 : hi // 4],
+                out=x_bf[c][:].rearrange("p (c i t) -> p c t i", t=PACK, i=4)[:, :, first : first + count],
+                in_=picked.rearrange("p (t c i) -> p c t i", t=PACK, i=4)[:, tokens, first : first + count],
             )
 
         def quantize_x(c):
             nc.vector.quantize_mx(out=x_w[c][:].bitcast(FP8X4), scales=x_s[c][:], in_=x_bf[c][:])
 
-        def first_layer(c):
-            lo, hi = FIRST[c]
-            for s in range(lo // SUB, hi // SUB):
-                cols = slice(s * SUB - lo, (s + 1) * SUB - lo)
-                ya[s] = bank_tile([P, PACK, SUB], 1 + (s - 1) % 3 if s else 0)
-                for t in range(PACK):
-                    rows = slice(t * P, (t + 1) * P)
-                    nc.tensor.matmul_mx(
-                        out=ya[s][:, t, :],
-                        lhsT=wa_w[:, rows].bitcast(FP8X4),
-                        lhsT_scale=wa_s[:, rows],
-                        rhs=x_w[c][:, cols].bitcast(FP8X4),
-                        rhs_scale=x_s[c][:, cols],
-                        start=True,
-                        stop=True,
-                    )
+        gather(0, 0, J)
+        x_plane.append(tile_at(0, [P, T], F32, "x_plane3"))
+        nc.sync.dma_start(out=x_plane[3][:], in_=x_rows[3])
+        wa_raw = tile_at(8, [P, PACK, R], F32, "wa_raw")
+        nc.sync.dma_start(out=wa_raw[:], in_=wa.rearrange("(p i) r -> p i r", i=PACK))
+        gather(1, 0, J)
+        for c in range(EARLY):
+            x_bf[c] = tile_at(36 + 2 * c, [P, CHUNK * PACK], BF16, "x_bf%d" % c)
+            weave_x(c, 0, 2)
+        gather(2, 0, J)
+        wd_w = tile_at(18, [P, N], I32, "wd_w")
+        nc.sync.dma_start(out=wd_w[:], in_=words_of(wd_words))
+        gather(3, 0, CHUNK)
+        gather(3, CHUNK, 3 * CHUNK)
+        bias = tile_at(20, [P, N // P], F32, "bias")
+        with nc.allow_non_contiguous_dma(reason="one bias value a partition"):
+            nc.sync.dma_start(out=bias[:], in_=b.rearrange("(t p) -> p t", p=P))
+        wd_s = tile_at(21, [P, N], U8, "wd_s")
+        place_scale_rows(nc.sync, wd_s, wd_scales[0])
 
-        def product(s):
-            c = max(k for k, chunk in enumerate(SECOND) if chunk[0] <= s * SUB)
-            first = (s * SUB - SECOND[c][0]) * PACK
-            nc.vector.tensor_tensor(
-                h_bf[c][:, first : first + SUB * PACK].rearrange("p (c t) -> p c t", t=PACK),
-                ya[s][:].rearrange("p t c -> p c t"),
-                yb[s][:].rearrange("p (c t) -> p c t", t=PACK),
-                MULT,
+        def round_wa(copy, h):
+            copy(
+                out=wa_bf[h].rearrange("p t (m i) -> p m i t", i=PACK),
+                in_=wa_raw[:].rearrange("p i (m t) -> p m i t", t=PACK)[:, :, :, 2 * h : 2 * h + 2],
             )
 
-        def quantize_h(c):
-            nc.vector.quantize_mx(out=h_w[c][:].bitcast(FP8X4), scales=h_s[c][:], in_=h_bf[c][:])
-
-        def second_layer(c, slices):
-            lo, hi = SECOND[c]
-            bank = bank_tile([P, len(slices), hi - lo], 4 + 2 * c + slices[0] // 2)
-            for v, t in enumerate(slices):
-                rows = slice(t * P, (t + 1) * P)
-                nc.tensor.matmul_mx(
-                    out=bank[:, v, :],
-                    lhsT=wd_w[:, rows].bitcast(FP8X4),
-                    lhsT_scale=wd_s[:, rows],
-                    rhs=h_w[c][:].bitcast(FP8X4),
-                    rhs_scale=h_s[c][:],
-                    start=True,
-                    stop=True,
-                )
-            return bank
-
-        def second_layer_by_halves(c, numbers):
-            slices_a_bank = N // P // len(numbers)
-            banks = [bank_tile([P, slices_a_bank, 2 * SUB], number) for number in numbers]
-            for half in range(2):
-                cols = slice(half * SUB, (half + 1) * SUB)
-                nc.vector.quantize_mx(
-                    out=h_w[c][:, cols].bitcast(FP8X4),
-                    scales=h_s[c][:, cols],
-                    in_=h_bf[c][:, half * SUB * PACK : (half + 1) * SUB * PACK],
-                )
-                for t in range(N // P):
-                    rows = slice(t * P, (t + 1) * P)
-                    nc.tensor.matmul_mx(
-                        out=banks[t // slices_a_bank][:, t % slices_a_bank, cols],
-                        lhsT=wd_w[:, rows].bitcast(FP8X4),
-                        lhsT_scale=wd_s[:, rows],
-                        rhs=h_w[c][:, cols].bitcast(FP8X4),
-                        rhs_scale=h_s[c][:, cols],
-                        start=True,
-                        stop=True,
-                    )
-            return [banks[t // slices_a_bank][:, t % slices_a_bank : t % slices_a_bank + 1, :] for t in range(N // P)]
-
-        def empty_and_store(c, slices, bank, on_scalar, queue):
-            lo, hi = SECOND[c]
-            result = tile([P, len(slices), hi - lo], F32, "result%d_%d" % (c, slices[0]))
-            for v, t in enumerate(slices):
-                if on_scalar:
-                    nc.scalar.activation(out=result[:, v, :], in_=bank[:, v, :], func=IDENTITY, bias=bias[:, t : t + 1])
-                else:
-                    nc.vector.tensor_scalar(result[:, v, :], bank[:, v, :], bias[:, t : t + 1], None, ADD)
-            queue.dma_start(out=out_rows[:, slices[0] : slices[-1] + 1, lo:hi], in_=result[:])
-
-        last = len(SECOND) - 1
-        interleave_x(0)
+        weave_x(0, 2, 2)
         quantize_x(0)
-        interleave_wa(nc.vector.tensor_copy, 0)
-        interleave_wa(nc.scalar.copy, 1)
+        round_wa(nc.vector.tensor_copy, 0)
+        round_wa(nc.scalar.copy, 1)
+        weave_x(1, 2, 2)
         wa_s = tile([P, R], U8, "wa_s")
         wa_w = tile([P, R], U32, "wa_w")
-        for h in range(2):
-            cols = slice(h * R // 2, (h + 1) * R // 2)
-            nc.vector.quantize_mx(out=wa_w[:, cols].bitcast(FP8X4), scales=wa_s[:, cols], in_=wa_bf[h])
-        first_layer(0)
-        interleave_x(1)
-        gather(3, PARTS[2:])
-        for c in range(2, len(FIRST)):
-            interleave_x(c)
-        copy_yb(J // SUB - 1, yb_bank, late.tile([P, SUB * PACK], F32, name="yb_last", offset=2048, align_bytes=64))
+        nc.vector.quantize_mx(out=wa_w[:, : 2 * P].bitcast(FP8X4), scales=wa_s[:, : 2 * P], in_=wa_bf[0].rearrange("p t w -> p (t w)"))
+        for t in (2, 3):
+            cols = slice(t * P, (t + 1) * P)
+            nc.vector.quantize_mx(out=wa_w[:, cols].bitcast(FP8X4), scales=wa_s[:, cols], in_=wa_bf[1][:, t - 2, :])
+
+        ya = {}
+        ya_share = {}
+
+        def project_x(s):
+            cols = slice(s % 2 * SUB, (s % 2 + 1) * SUB)
+            ya[s] = first_layer(YA_BANKS[s], wa_w, wa_s, x_w[s // 2][:, cols], x_s[s // 2][:, cols])
+
+        def copy_share(c):
+            ya_share[c] = tile([P, SHARE, PACK], F32, "ya_share%d" % c)
+            nc.scalar.activation(out=ya_share[c][:], in_=ya[2 * c][:, :, SUB - SHARE :].rearrange("p t c -> p c t"), func=IDENTITY)
+
+        def weave_whole(c):
+            x_bf[c] = tile_at(8 + 2 * (c - EARLY), [P, CHUNK * PACK], BF16, "x_bf%d" % c)
+            weave_x(c, 0, PACK)
+
+        project_x(0)
+        project_x(1)
+        gather(3, 3 * CHUNK, J)
         quantize_x(1)
-        first_layer(1)
-        for s in range(J // SUB):
-            product(s)
-            for c, (lo, hi) in enumerate(FIRST[2:], 2):
-                if lo == (s + 3) * SUB:
-                    quantize_x(c)
-                    first_layer(c)
-            for c, (lo, hi) in enumerate(SECOND):
-                if c < last - 1 and hi == (s + 1) * SUB:
-                    quantize_h(c)
-                    for slices in ((0, 1), (2, 3)):
-                        bank = second_layer(c, slices)
-                        for v, t in enumerate(slices):
-                            empty_and_store(c, (t,), bank[:, v : v + 1, :], True, nc.sync)
-                if c == last - 1 and hi == (s + 1) * SUB:
-                    for t, bank in enumerate(second_layer_by_halves(c, (0, 2))):
-                        empty_and_store(c, (t,), bank, True, nc.sync)
-        for t, bank in enumerate(second_layer_by_halves(last, (4, 5, 6, 7))):
-            empty_and_store(last, (t,), bank, t % 2 == 1, nc.scalar if t == N // P - 1 else nc.sync)
+        project_x(2)
+        project_x(3)
+        weave_whole(2)
+        copy_share(1)
+        weave_whole(3)
+
+        out_rows = out.rearrange("(t p) j -> p t j", p=P)
+        h_bf = {}
+        h_w = [tile([P, SUB], U32, "h_w%d" % s) for s in range(J // SUB)]
+        h_s = [tile([P, SUB], U8, "h_s%d" % s) for s in range(J // SUB)]
+
+        def product(s, slot, tokens):
+            h_bf[s] = tile_at(slot, [P, SUB, PACK], BF16, "h_bf%d" % s)
+            if tokens < SUB:
+                nc.gpsimd.tensor_tensor(h_bf[s][:, tokens:], ya_share[s // 2][:], yb[s][:, tokens:], MULT)
+            nc.vector.tensor_tensor(h_bf[s][:, :tokens], ya[s][:, :, :tokens].rearrange("p t c -> p c t"), yb[s][:, :tokens], MULT)
+
+        def second_layer(order, numbers):
+            a_bank = N // P // len(numbers)
+            banks = [bank_tile([P, a_bank, CHUNK], number) for number in numbers]
+            for s in order:
+                nc.vector.quantize_mx(out=h_w[s][:].bitcast(FP8X4), scales=h_s[s][:], in_=h_bf[s][:].rearrange("p c t -> p (c t)"))
+                for t in range(N // P):
+                    rows = slice(t * P, (t + 1) * P)
+                    mx(banks[t // a_bank][:, t % a_bank, s % 2 * SUB : (s % 2 + 1) * SUB], wd_w[:, rows], wd_s[:, rows], h_w[s][:], h_s[s][:])
+            return [banks[t // a_bank][:, t % a_bank, :] for t in range(N // P)]
+
+        def empty_and_store(c, t, bank, on_scalar, queue):
+            result = tile([P, CHUNK], F32, "result%d_%d" % (c, t))
+            if on_scalar:
+                nc.scalar.activation(out=result[:], in_=bank, func=IDENTITY, bias=bias[:, t : t + 1])
+            else:
+                nc.vector.tensor_scalar(result[:], bank, bias[:, t : t + 1], None, ADD)
+            queue.dma_start(out=out_rows[:, t, c * CHUNK : (c + 1) * CHUNK], in_=result[:])
+
+        last = CHUNKS - 1
+        for c in range(CHUNKS):
+            order = (2 * c + 1, 2 * c) if c else (0, 1)
+            product(order[0], H_KIB[c], SUB)
+            product(order[1], H_KIB[c - 1], SUB - SHARE if c else SUB)
+            ahead = c + EARLY
+            if ahead < CHUNKS:
+                quantize_x(ahead)
+                project_x(2 * ahead)
+            banks = second_layer(order, OUT_BANKS[c])
+            if ahead < CHUNKS:
+                copy_share(ahead)
+                project_x(2 * ahead + 1)
+            for t, bank in enumerate(banks):
+                empty_and_store(c, t, bank, c < last or t % 2 == 1, nc.sync)

@@ -28,15 +28,16 @@ KIB = 1024
 CHUNKS = J // CHUNK
 EARLY = 2
 RING = 4
+PIECES = ((0, 256), (256, 384), (384, 512), (512, 768), (768, 1024))
 SHARE = 48
-H_KIB = (38, 42, 43, 44, 39)
+H_KIB = (48, 52, 53, 54, 49)
 YA_BANKS = (0, 1, 2, 3, 0, 3, 2, 1)
 OUT_BANKS = ((4, 5), (6, 7), (4, 5), (6, 7, 0, 3))
 
 
-def place_scale_rows(queue, plane, rows):
+def place_scale_rows(queues, plane, rows):
     for q in range(4):
-        queue.dma_start(out=plane[q:P:32, :].bitcast(I32), in_=rows[q:16:4, :].bitcast(I32))
+        queues[q % len(queues)].dma_start(out=plane[q:P:32, :].bitcast(I32), in_=rows[q:16:4, :].bitcast(I32))
 
 
 def words_of(packed):
@@ -111,20 +112,20 @@ def tile_list_htabg_mul_bias_kernel(tc, tab_words, tab_scales, xT, wgt2, wa, wb_
 
         v_rows = tile_at(25, [P, J], U8, "v_rows")
         nc.vector.tensor_copy(v_rows[:], tab_s[:].indirect(tab_list[:]))
-        both_rows = tile_at(26, [P, J + R], U8, "both_rows")
+        both_rows = tile_at(34, [P, J + R], U8, "both_rows")
         nc.vector.tensor_copy(both_rows[96:P, :J].bitcast(I32), v_rows[96:P, :].bitcast(I32))
         nc.gpsimd.tensor_copy(
             out=both_rows[:, J:].rearrange("p (t c i) -> p c t i", t=PACK, i=16),
             in_=wb_s[:].rearrange("p (c i t) -> p c t i", t=PACK, i=16),
         )
         both_s = tile([P, J + R], U8, "both_s")
-        place_scale_rows(nc.sync, both_s, both_rows[STAGE:P, :])
+        place_scale_rows((nc.sync, nc.scalar), both_s, both_rows[STAGE:P, :])
         v_s = both_s[:, :J]
         wbp_s = both_s[:, J:]
         x_plane.append(tile_at(18, [P, T], F32, "x_plane1"))
         nc.sync.dma_start(out=x_plane[1][:], in_=x_rows[1])
 
-        v_w = tile_at(37, [P, J], U32, "v_w")
+        v_w = tile_at(47, [P, J], U32, "v_w")
         nc.vector.tensor_copy(v_w[:], tab_w[:].bitcast(U32).indirect(tab_list[:]))
         x_plane.append(tile_at(27, [P, T], F32, "x_plane2"))
         nc.sync.dma_start(out=x_plane[2][:], in_=x_rows[2])
@@ -151,8 +152,8 @@ def tile_list_htabg_mul_bias_kernel(tc, tab_words, tab_scales, xT, wgt2, wa, wb_
 
         picked = tile([P, PACK * J], F32, "picked")[:]
         wa_bf = [
-            tile([P, 2, R], BF16, "wa_bf0")[:],
-            picked[:, 3 * J :].bitcast(BF16).rearrange("p (c w) -> p c w", c=CHUNKS)[:, 0 : CHUNKS : CHUNKS - 1],
+            tile([P, 2, 2, R // 2], BF16, "wa_bf0")[:],
+            picked[:, 3 * J :].bitcast(BF16).rearrange("p (c u w) -> p c u w", c=CHUNKS, u=2)[:, 0 : CHUNKS : CHUNKS - 1],
         ]
 
         def gather(i, lo, hi):
@@ -167,25 +168,28 @@ def tile_list_htabg_mul_bias_kernel(tc, tab_words, tab_scales, xT, wgt2, wa, wb_
         x_w = [tile_at(10, [P, CHUNK], U32, "x_w1") if c == 1 else tile([P, CHUNK], U32, "x_w%d" % c) for c in range(CHUNKS)]
         x_s = [tile([P, CHUNK], U8, "x_s%d" % c) for c in range(CHUNKS)]
 
-        def weave_x(c, first, count):
-            tokens = slice(c * CHUNK // 4, (c + 1) * CHUNK // 4)
+        def weave_x(piece, first, count):
+            lo, hi = PIECES[piece]
             nc.scalar.copy(
-                out=x_bf[c][:].rearrange("p (c i t) -> p c t i", t=PACK, i=4)[:, :, first : first + count],
-                in_=picked.rearrange("p (t c i) -> p c t i", t=PACK, i=4)[:, tokens, first : first + count],
+                out=x_bf[piece][:].rearrange("p (c i t) -> p c t i", t=PACK, i=4)[:, :, first : first + count],
+                in_=picked.rearrange("p (t c i) -> p c t i", t=PACK, i=4)[:, lo // 4 : hi // 4, first : first + count],
             )
 
-        def quantize_x(c):
-            nc.vector.quantize_mx(out=x_w[c][:].bitcast(FP8X4), scales=x_s[c][:], in_=x_bf[c][:])
+        def quantize_x(piece):
+            lo, hi = PIECES[piece]
+            c = lo // CHUNK
+            cols = slice(lo - c * CHUNK, hi - c * CHUNK)
+            nc.vector.quantize_mx(out=x_w[c][:, cols].bitcast(FP8X4), scales=x_s[c][:, cols], in_=x_bf[piece][:])
 
-        gather(0, 0, J)
-        x_plane.append(tile_at(0, [P, T], F32, "x_plane3"))
+        x_plane.append(tile_at(35, [P, T], F32, "x_plane3"))
         nc.sync.dma_start(out=x_plane[3][:], in_=x_rows[3])
+        gather(0, 0, J)
         wa_raw = tile_at(8, [P, PACK, R], F32, "wa_raw")
         nc.sync.dma_start(out=wa_raw[:], in_=wa.rearrange("(p i) r -> p i r", i=PACK))
         gather(1, 0, J)
-        for c in range(EARLY):
-            x_bf[c] = tile_at(36 + 2 * c, [P, CHUNK * PACK], BF16, "x_bf%d" % c)
-            weave_x(c, 0, 2)
+        for piece, (lo, hi) in enumerate(PIECES[: EARLY + 1]):
+            x_bf[piece] = tile_at(46 + lo // SUB, [P, (hi - lo) * PACK], BF16, "x_bf%d" % piece)
+            weave_x(piece, 0, 2)
         gather(2, 0, J)
         wd_w = tile_at(18, [P, N], I32, "wd_w")
         nc.sync.dma_start(out=wd_w[:], in_=words_of(wd_words))
@@ -195,12 +199,12 @@ def tile_list_htabg_mul_bias_kernel(tc, tab_words, tab_scales, xT, wgt2, wa, wb_
         with nc.allow_non_contiguous_dma(reason="one bias value a partition"):
             nc.sync.dma_start(out=bias[:], in_=b.rearrange("(t p) -> p t", p=P))
         wd_s = tile_at(21, [P, N], U8, "wd_s")
-        place_scale_rows(nc.sync, wd_s, wd_scales[0])
+        place_scale_rows((nc.sync,), wd_s, wd_scales[0])
 
         def round_wa(copy, h):
             copy(
-                out=wa_bf[h].rearrange("p t (m i) -> p m i t", i=PACK),
-                in_=wa_raw[:].rearrange("p i (m t) -> p m i t", t=PACK)[:, :, :, 2 * h : 2 * h + 2],
+                out=wa_bf[h].rearrange("p c u (m i) -> p m i c u", i=PACK),
+                in_=wa_raw[:, :, h * R // 2 : (h + 1) * R // 2].rearrange("p i (m c u) -> p m i c u", c=2, u=2),
             )
 
         weave_x(0, 2, 2)
@@ -208,12 +212,13 @@ def tile_list_htabg_mul_bias_kernel(tc, tab_words, tab_scales, xT, wgt2, wa, wb_
         round_wa(nc.vector.tensor_copy, 0)
         round_wa(nc.scalar.copy, 1)
         weave_x(1, 2, 2)
+        weave_x(2, 2, 2)
         wa_s = tile([P, R], U8, "wa_s")
         wa_w = tile([P, R], U32, "wa_w")
-        nc.vector.quantize_mx(out=wa_w[:, : 2 * P].bitcast(FP8X4), scales=wa_s[:, : 2 * P], in_=wa_bf[0].rearrange("p t w -> p (t w)"))
-        for t in (2, 3):
-            cols = slice(t * P, (t + 1) * P)
-            nc.vector.quantize_mx(out=wa_w[:, cols].bitcast(FP8X4), scales=wa_s[:, cols], in_=wa_bf[1][:, t - 2, :])
+        for h in range(2):
+            for t in range(PACK):
+                cols = slice(t * P + h * P // 2, t * P + (h + 1) * P // 2)
+                nc.vector.quantize_mx(out=wa_w[:, cols].bitcast(FP8X4), scales=wa_s[:, cols], in_=wa_bf[h][:, t // 2, t % 2, :])
 
         ya = {}
         ya_share = {}
@@ -227,14 +232,15 @@ def tile_list_htabg_mul_bias_kernel(tc, tab_words, tab_scales, xT, wgt2, wa, wb_
             nc.scalar.activation(out=ya_share[c][:], in_=ya[2 * c][:, :, SUB - SHARE :].rearrange("p t c -> p c t"), func=IDENTITY)
 
         def weave_whole(c):
-            x_bf[c] = tile_at(8 + 2 * (c - EARLY), [P, CHUNK * PACK], BF16, "x_bf%d" % c)
-            weave_x(c, 0, PACK)
+            x_bf[c + 1] = tile_at(8 + 2 * (c - EARLY), [P, CHUNK * PACK], BF16, "x_bf%d" % (c + 1))
+            weave_x(c + 1, 0, PACK)
 
         project_x(0)
         project_x(1)
         gather(3, 3 * CHUNK, J)
         quantize_x(1)
         project_x(2)
+        quantize_x(2)
         project_x(3)
         weave_whole(2)
         copy_share(1)
@@ -276,7 +282,7 @@ def tile_list_htabg_mul_bias_kernel(tc, tab_words, tab_scales, xT, wgt2, wa, wb_
             product(order[1], H_KIB[c - 1], SUB - SHARE if c else SUB)
             ahead = c + EARLY
             if ahead < CHUNKS:
-                quantize_x(ahead)
+                quantize_x(ahead + 1)
                 project_x(2 * ahead)
             banks = second_layer(order, OUT_BANKS[c])
             if ahead < CHUNKS:

@@ -152,8 +152,8 @@ def tile_list_htabg_mul_bias_kernel(tc, tab_words, tab_scales, xT, wgt2, wa, wb_
 
         picked = tile([P, PACK * J], F32, "picked")[:]
         wa_bf = [
-            tile([P, 2, 2, R // 2], BF16, "wa_bf0")[:],
-            picked[:, 3 * J :].bitcast(BF16).rearrange("p (c u w) -> p c u w", c=CHUNKS, u=2)[:, 0 : CHUNKS : CHUNKS - 1],
+            tile([P, 2, R], BF16, "wa_bf0")[:],
+            picked[:, 3 * J :].bitcast(BF16).rearrange("p (c w) -> p c w", c=CHUNKS)[:, 0 : CHUNKS : CHUNKS - 1],
         ]
 
         def gather(i, lo, hi):
@@ -203,8 +203,8 @@ def tile_list_htabg_mul_bias_kernel(tc, tab_words, tab_scales, xT, wgt2, wa, wb_
 
         def round_wa(copy, h):
             copy(
-                out=wa_bf[h].rearrange("p c u (m i) -> p m i c u", i=PACK),
-                in_=wa_raw[:, :, h * R // 2 : (h + 1) * R // 2].rearrange("p i (m c u) -> p m i c u", c=2, u=2),
+                out=wa_bf[h].rearrange("p t (m i) -> p m i t", i=PACK),
+                in_=wa_raw[:].rearrange("p i (m t) -> p m i t", t=PACK)[:, :, :, 2 * h : 2 * h + 2],
             )
 
         weave_x(0, 2, 2)
@@ -215,10 +215,10 @@ def tile_list_htabg_mul_bias_kernel(tc, tab_words, tab_scales, xT, wgt2, wa, wb_
         weave_x(2, 2, 2)
         wa_s = tile([P, R], U8, "wa_s")
         wa_w = tile([P, R], U32, "wa_w")
-        for h in range(2):
-            for t in range(PACK):
-                cols = slice(t * P + h * P // 2, t * P + (h + 1) * P // 2)
-                nc.vector.quantize_mx(out=wa_w[:, cols].bitcast(FP8X4), scales=wa_s[:, cols], in_=wa_bf[h][:, t // 2, t % 2, :])
+        nc.vector.quantize_mx(out=wa_w[:, : 2 * P].bitcast(FP8X4), scales=wa_s[:, : 2 * P], in_=wa_bf[0].rearrange("p t w -> p (t w)"))
+        for t in (2, 3):
+            cols = slice(t * P, (t + 1) * P)
+            nc.vector.quantize_mx(out=wa_w[:, cols].bitcast(FP8X4), scales=wa_s[:, cols], in_=wa_bf[1][:, t - 2, :])
 
         ya = {}
         ya_share = {}

@@ -55,7 +55,7 @@ def tile_list_htabg_mul_bias_kernel(tc, tab_words, tab_scales, xT, wgt2, wa, wb_
             return keep.tile(shape, dtype, name=name, tag=slot or name, align_bytes=64)
 
         def tile_at(kib, shape, dtype, name):
-            return laid.tile(shape, dtype, name=name, offset=kib * KIB, align_bytes=64)
+            return laid.tile(shape, dtype, name=name, offset=int(kib * KIB), align_bytes=64)
 
         def bank_tile(shape, number):
             return psum.tile(shape, F32, name="bank%d" % number)
@@ -76,7 +76,7 @@ def tile_list_htabg_mul_bias_kernel(tc, tab_words, tab_scales, xT, wgt2, wa, wb_
         tab_s = tile([P, T], U8, "tab_s")
         tab_w = tile([P, T], I32, "tab_w", "slot_tab")
         wb_w = tile([P, R], I32, "wb_w", "slot_wb")
-        wb_s = tile_at(24, [P, R], U8, "wb_s")
+        wb_s = tile_at(25, [P, R], U8, "wb_s")
         wgt = tile([P, J], F32, "wgt")
         head_w = tile([P, P], F32, "head_w")
         identity = tile([P, P], F32, "identity")
@@ -110,7 +110,7 @@ def tile_list_htabg_mul_bias_kernel(tc, tab_words, tab_scales, xT, wgt2, wa, wb_
                 nc.tensor.transpose(turned[:, c, :], spread[:, PACK * u + c, :], identity[:])
             nc.scalar.copy(out=wgt[:, u * PACK * P : (u + 1) * PACK * P], in_=turned[:].rearrange("p c v -> p (c v)"))
 
-        v_rows = tile_at(25, [P, J], U8, "v_rows")
+        v_rows = tile_at(24, [P, J], U8, "v_rows")
         nc.vector.tensor_copy(v_rows[:], tab_s[:].indirect(tab_list[:]))
         both_rows = tile_at(34, [P, J + R], U8, "both_rows")
         nc.vector.tensor_copy(both_rows[96:P, :J].bitcast(I32), v_rows[96:P, :].bitcast(I32))
@@ -119,15 +119,15 @@ def tile_list_htabg_mul_bias_kernel(tc, tab_words, tab_scales, xT, wgt2, wa, wb_
             in_=wb_s[:].rearrange("p (c i t) -> p c t i", t=PACK, i=16),
         )
         both_s = tile([P, J + R], U8, "both_s")
-        place_scale_rows((nc.sync, nc.scalar), both_s, both_rows[STAGE:P, :])
+        place_scale_rows((nc.sync,), both_s, both_rows[STAGE:P, :])
         v_s = both_s[:, :J]
         wbp_s = both_s[:, J:]
-        x_plane.append(tile_at(18, [P, T], F32, "x_plane1"))
+        x_plane.append(tile_at(17.25, [P, T], F32, "x_plane1"))
         nc.sync.dma_start(out=x_plane[1][:], in_=x_rows[1])
 
         v_w = tile_at(47, [P, J], U32, "v_w")
         nc.vector.tensor_copy(v_w[:], tab_w[:].bitcast(U32).indirect(tab_list[:]))
-        x_plane.append(tile_at(27, [P, T], F32, "x_plane2"))
+        x_plane.append(tile_at(25.25, [P, T], F32, "x_plane2"))
         nc.sync.dma_start(out=x_plane[2][:], in_=x_rows[2])
 
         wbp_w = tile([P, R], I32, "wbp_w")

@@ -28,11 +28,12 @@ KIB = 1024
 CHUNKS = J // CHUNK
 EARLY = 2
 RING = 4
+HELP = 96
 PIECES = ((0, 256), (256, 384), (384, 512), (512, 768), (768, 1024))
 SHARE = 48
 H_KIB = (48, 52, 53, 54, 49)
-YA_BANKS = (0, 1, 2, 3, 0, 3, 2, 1)
-OUT_BANKS = ((4, 5), (6, 7), (4, 5), (6, 7, 0, 3))
+YA_BANKS = (0, 1, 2, 3, 0, 1, 2, 3)
+OUT_BANKS = ((4, 5), (6, 7), (4, 5), (6, 7, 0, 1))
 
 
 def place_scale_rows(queues, plane, rows):
@@ -125,8 +126,9 @@ def tile_list_htabg_mul_bias_kernel(tc, tab_words, tab_scales, xT, wgt2, wa, wb_
         x_plane.append(tile_at(17.25, [P, T], F32, "x_plane1"))
         nc.sync.dma_start(out=x_plane[1][:], in_=x_rows[1])
 
-        v_w = tile_at(47, [P, J], U32, "v_w")
-        nc.vector.tensor_copy(v_w[:], tab_w[:].bitcast(U32).indirect(tab_list[:]))
+        v_w = [tile([P, J // 2], U32, "v_w0"), tile_at(47.5, [P, J // 2], U32, "v_w1")]
+        for h in range(2):
+            nc.vector.tensor_copy(v_w[h][:], tab_w[:].bitcast(U32).indirect(tab_list[:, h * J // 32 : (h + 1) * J // 32]))
         x_plane.append(tile_at(25.25, [P, T], F32, "x_plane2"))
         nc.sync.dma_start(out=x_plane[2][:], in_=x_rows[2])
 
@@ -146,7 +148,7 @@ def tile_list_htabg_mul_bias_kernel(tc, tab_words, tab_scales, xT, wgt2, wa, wb_
         yb = []
         for s in range(J // SUB):
             cols = slice(s * SUB, (s + 1) * SUB)
-            acc = first_layer(s % RING, wbp_w, wbp_s, v_w[:, cols], v_s[:, cols])
+            acc = first_layer(s % RING, wbp_w, wbp_s, v_w[s // RING][:, s % RING * SUB : (s % RING + 1) * SUB], v_s[:, cols])
             yb.append(tile([P, SUB, PACK], F32, "yb%d" % s))
             nc.scalar.activation(out=yb[s][:], in_=acc[:].rearrange("p t c -> p c t"), func=IDENTITY)
 
@@ -165,39 +167,43 @@ def tile_list_htabg_mul_bias_kernel(tc, tab_words, tab_scales, xT, wgt2, wa, wb_
             )
 
         x_bf = {}
-        x_w = [tile_at(10, [P, CHUNK], U32, "x_w1") if c == 1 else tile([P, CHUNK], U32, "x_w%d" % c) for c in range(CHUNKS)]
+        x_w = [tile([P, CHUNK], U32, "x_w%d" % c) for c in range(CHUNKS)]
         x_s = [tile([P, CHUNK], U8, "x_s%d" % c) for c in range(CHUNKS)]
 
-        def weave_x(piece, first, count):
+        def weave_x(piece, first, count, skip=0):
             lo, hi = PIECES[piece]
             nc.scalar.copy(
-                out=x_bf[piece][:].rearrange("p (c i t) -> p c t i", t=PACK, i=4)[:, :, first : first + count],
-                in_=picked.rearrange("p (t c i) -> p c t i", t=PACK, i=4)[:, lo // 4 : hi // 4, first : first + count],
+                out=x_bf[piece].rearrange("p (c i t) -> p c t i", t=PACK, i=4)[:, skip // 4 :, first : first + count],
+                in_=picked.rearrange("p (t c i) -> p c t i", t=PACK, i=4)[:, (lo + skip) // 4 : hi // 4, first : first + count],
             )
 
         def quantize_x(piece):
             lo, hi = PIECES[piece]
             c = lo // CHUNK
             cols = slice(lo - c * CHUNK, hi - c * CHUNK)
-            nc.vector.quantize_mx(out=x_w[c][:, cols].bitcast(FP8X4), scales=x_s[c][:, cols], in_=x_bf[piece][:])
+            nc.vector.quantize_mx(out=x_w[c][:, cols].bitcast(FP8X4), scales=x_s[c][:, cols], in_=x_bf[piece])
 
         x_plane.append(tile_at(35, [P, T], F32, "x_plane3"))
         nc.sync.dma_start(out=x_plane[3][:], in_=x_rows[3])
         gather(0, 0, J)
+        bias_rows = tile_at(4, [P, P], F32, "bias_rows")
+        nc.gpsimd.memset(bias_rows[: P - PACK, :], 0.0)
+        nc.sync.dma_start(out=bias_rows[P - PACK :, :], in_=b.rearrange("(t p) -> t p", p=P))
         wa_raw = tile_at(8, [P, PACK, R], F32, "wa_raw")
         nc.sync.dma_start(out=wa_raw[:], in_=wa.rearrange("(p i) r -> p i r", i=PACK))
         gather(1, 0, J)
         for piece, (lo, hi) in enumerate(PIECES[: EARLY + 1]):
-            x_bf[piece] = tile_at(46 + lo // SUB, [P, (hi - lo) * PACK], BF16, "x_bf%d" % piece)
+            x_bf[piece] = tile_at(46 + lo // SUB, [P, CHUNK * PACK if piece == EARLY else (hi - lo) * PACK], BF16, "x_bf%d" % piece)[:, : (hi - lo) * PACK]
             weave_x(piece, 0, 2)
         gather(2, 0, J)
         wd_w = tile_at(18, [P, N], I32, "wd_w")
         nc.sync.dma_start(out=wd_w[:], in_=words_of(wd_words))
         gather(3, 0, CHUNK)
         gather(3, CHUNK, 3 * CHUNK)
-        bias = tile_at(20, [P, N // P], F32, "bias")
-        with nc.allow_non_contiguous_dma(reason="one bias value a partition"):
-            nc.sync.dma_start(out=bias[:], in_=b.rearrange("(t p) -> p t", p=P))
+        bias = tile([P, N // P], F32, "bias")
+        bias_turned = bank_tile([P, P], 7)
+        nc.tensor.transpose(bias_turned[:], bias_rows[:], identity[:])
+        nc.scalar.copy(out=bias[:], in_=bias_turned[:, P - PACK :])
         wd_s = tile_at(21, [P, N], U8, "wd_s")
         place_scale_rows((nc.sync,), wd_s, wd_scales[0])
 
@@ -231,9 +237,6 @@ def tile_list_htabg_mul_bias_kernel(tc, tab_words, tab_scales, xT, wgt2, wa, wb_
             ya_share[c] = tile([P, SHARE, PACK], F32, "ya_share%d" % c)
             nc.scalar.activation(out=ya_share[c][:], in_=ya[2 * c][:, :, SUB - SHARE :].rearrange("p t c -> p c t"), func=IDENTITY)
 
-        def weave_whole(c):
-            x_bf[c + 1] = tile_at(8 + 2 * (c - EARLY), [P, CHUNK * PACK], BF16, "x_bf%d" % (c + 1))
-            weave_x(c + 1, 0, PACK)
 
         project_x(0)
         project_x(1)
@@ -242,9 +245,19 @@ def tile_list_htabg_mul_bias_kernel(tc, tab_words, tab_scales, xT, wgt2, wa, wb_
         project_x(2)
         quantize_x(2)
         project_x(3)
-        weave_whole(2)
+        x_bf[3] = tile_at(8, [P, CHUNK * PACK], BF16, "x_bf3")[:]
+        weave_x(3, 0, PACK)
         copy_share(1)
-        weave_whole(3)
+        x_bf[4] = tile_at(50, [P, CHUNK * PACK], BF16, "x_bf4")[:]
+        nc.gpsimd.tensor_scalar(
+            x_bf[4][:, : HELP * PACK].rearrange("p (c t) -> p c t", t=PACK),
+            picked.rearrange("p (t c) -> p c t", t=PACK)[:, 3 * CHUNK : 3 * CHUNK + HELP],
+            1.0,
+            0.0,
+            MULT,
+            ADD,
+        )
+        weave_x(4, 0, PACK, HELP)
 
         out_rows = out.rearrange("(t p) j -> p t j", p=P)
         h_bf = {}

@@ -112,9 +112,12 @@ def tile_list_htabg_mul_bias_kernel(tc, tab_words, tab_scales, xT, wgt2, wa, wb_
             nc.scalar.copy(out=wgt[:, u * PACK * P : (u + 1) * PACK * P], in_=turned[:].rearrange("p c v -> p (c v)"))
 
         v_rows = tile_at(24, [P, J], U8, "v_rows")
-        nc.vector.tensor_copy(v_rows[:], tab_s[:].indirect(tab_list[:]))
+        halves = [slice(h * J // 2, (h + 1) * J // 2) for h in range(2)]
+        for h in range(2):
+            nc.vector.tensor_copy(v_rows[:, halves[h]], tab_s[:].indirect(tab_list[:, h * J // 32 : (h + 1) * J // 32]))
         both_rows = tile_at(34, [P, J + R], U8, "both_rows")
-        nc.vector.tensor_copy(both_rows[96:P, :J].bitcast(I32), v_rows[96:P, :].bitcast(I32))
+        for h in range(2):
+            nc.vector.tensor_copy(both_rows[96:P, halves[h]].bitcast(I32), v_rows[96:P, halves[h]].bitcast(I32))
         nc.gpsimd.tensor_copy(
             out=both_rows[:, J:].rearrange("p (t c i) -> p c t i", t=PACK, i=16),
             in_=wb_s[:].rearrange("p (c i t) -> p c t i", t=PACK, i=16),
@@ -154,7 +157,7 @@ def tile_list_htabg_mul_bias_kernel(tc, tab_words, tab_scales, xT, wgt2, wa, wb_
 
         picked = tile([P, PACK * J], F32, "picked")[:]
         wa_bf = [
-            tile([P, 2, R], BF16, "wa_bf0")[:],
+            None,
             picked[:, 3 * J :].bitcast(BF16).rearrange("p (c w) -> p c w", c=CHUNKS)[:, 0 : CHUNKS : CHUNKS - 1],
         ]
 
@@ -207,21 +210,26 @@ def tile_list_htabg_mul_bias_kernel(tc, tab_words, tab_scales, xT, wgt2, wa, wb_
         wd_s = tile_at(21, [P, N], U8, "wd_s")
         place_scale_rows((nc.sync,), wd_s, wd_scales[0])
 
-        def round_wa(copy, h):
+        def round_wa(copy, rounded, h, channels):
             copy(
-                out=wa_bf[h].rearrange("p t (m i) -> p m i t", i=PACK),
-                in_=wa_raw[:].rearrange("p i (m t) -> p m i t", t=PACK)[:, :, :, 2 * h : 2 * h + 2],
+                out=rounded.rearrange("p t (m i) -> p m i t", i=PACK),
+                in_=wa_raw[:].rearrange("p i (m t) -> p m i t", t=PACK)[:, channels, :, 2 * h : 2 * h + 2],
             )
 
         weave_x(0, 2, 2)
         quantize_x(0)
-        round_wa(nc.vector.tensor_copy, 0)
-        round_wa(nc.scalar.copy, 1)
+        wa_low = [tile([P, 2, R // 2], BF16, "wa_low%d" % u) for u in range(2)]
+        for u in range(2):
+            round_wa(nc.vector.tensor_copy, wa_low[u][:], 0, slice(u * P // 2, (u + 1) * P // 2))
+        round_wa(nc.scalar.copy, wa_bf[1], 1, slice(0, P))
         weave_x(1, 2, 2)
         weave_x(2, 2, 2)
         wa_s = tile([P, R], U8, "wa_s")
         wa_w = tile([P, R], U32, "wa_w")
-        nc.vector.quantize_mx(out=wa_w[:, : 2 * P].bitcast(FP8X4), scales=wa_s[:, : 2 * P], in_=wa_bf[0].rearrange("p t w -> p (t w)"))
+        for u in range(2):
+            for t in range(2):
+                cols = slice(t * P + u * P // 2, t * P + (u + 1) * P // 2)
+                nc.vector.quantize_mx(out=wa_w[:, cols].bitcast(FP8X4), scales=wa_s[:, cols], in_=wa_low[u][:, t, :])
         for t in (2, 3):
             cols = slice(t * P, (t + 1) * P)
             nc.vector.quantize_mx(out=wa_w[:, cols].bitcast(FP8X4), scales=wa_s[:, cols], in_=wa_bf[1][:, t - 2, :])

@@ -30,8 +30,8 @@ EARLY = 2
 RING = 4
 HELP = 96
 PIECES = ((0, 256), (256, 384), (384, 512), (512, 768), (768, 1024))
-SHARE = 48
-H_KIB = (48, 52, 53, 54, 49)
+SHARE = 56
+H_KIB = (47.5, 52, 53, 54, 48.5)
 YA_BANKS = (0, 1, 2, 3, 0, 1, 2, 3)
 OUT_BANKS = ((4, 5), (6, 7), (4, 5), (6, 7, 0, 1))
 
@@ -196,7 +196,7 @@ def tile_list_htabg_mul_bias_kernel(tc, tab_words, tab_scales, xT, wgt2, wa, wb_
         nc.sync.dma_start(out=wa_raw[:], in_=wa.rearrange("(p i) r -> p i r", i=PACK))
         gather(1, 0, J)
         for piece, (lo, hi) in enumerate(PIECES[: EARLY + 1]):
-            x_bf[piece] = tile_at(46 + lo // SUB, [P, CHUNK * PACK if piece == EARLY else (hi - lo) * PACK], BF16, "x_bf%d" % piece)[:, : (hi - lo) * PACK]
+            x_bf[piece] = tile_at(46 + lo // SUB, [P, (hi - lo) * PACK], BF16, "x_bf%d" % piece)[:]
             weave_x(piece, 0, 2)
         gather(2, 0, J)
         wd_w = tile_at(18, [P, N], I32, "wd_w")
@@ -256,7 +256,7 @@ def tile_list_htabg_mul_bias_kernel(tc, tab_words, tab_scales, xT, wgt2, wa, wb_
         x_bf[3] = tile_at(8, [P, CHUNK * PACK], BF16, "x_bf3")[:]
         weave_x(3, 0, PACK)
         copy_share(1)
-        x_bf[4] = tile_at(50, [P, CHUNK * PACK], BF16, "x_bf4")[:]
+        x_bf[4] = tile_at(49.5, [P, CHUNK * PACK], BF16, "x_bf4")[:]
         nc.gpsimd.tensor_scalar(
             x_bf[4][:, : HELP * PACK].rearrange("p (c t) -> p c t", t=PACK),
             picked.rearrange("p (t c) -> p c t", t=PACK)[:, 3 * CHUNK : 3 * CHUNK + HELP],

from contextlib import ExitStack

import concourse.mybir as mybir
from concourse.masks import make_identity

K, L, R, N, T, J = 512, 512, 512, 512, 2048, 1024
FLOPS = 2 * J * (K * R + L * R + R * N)

F32 = mybir.dt.float32
BF16 = mybir.dt.bfloat16
I32 = mybir.dt.int32
U32 = mybir.dt.uint32
U16 = mybir.dt.uint16
U8 = mybir.dt.uint8
FP8X4 = mybir.dt.float8_e4m3fn_x4
MULT = mybir.AluOpType.mult
ADD = mybir.AluOpType.add
IDENTITY = mybir.ActivationFunctionType.Identity

P = 128
PACK = 4
SUB = 128
CHUNK = 256
STAGE = 112
HEADS = 8
RUN = J // P
KIB = 1024
CHUNKS = J // CHUNK
EARLY = 2
RING = 4
HELP = 96
PIECES = ((0, 256), (256, 384), (384, 512), (512, 768), (768, 1024))
SHARE = 56
H_KIB = (47.5, 52, 53, 54, 48.5)
YA_BANKS = (0, 1, 2, 3, 0, 1, 2, 3)
OUT_BANKS = ((4, 5), (6, 7), (4, 5), (6, 7, 0, 1))


def place_scale_rows(queues, plane, rows):
    for q in range(4):
        queues[q % len(queues)].dma_start(out=plane[q:P:32, :].bitcast(I32), in_=rows[q:16:4, :].bitcast(I32))


def words_of(packed):
    return packed[0].rearrange("p c i -> p (c i)").bitcast(I32)


def tile_list_htabg_mul_bias_kernel(tc, tab_words, tab_scales, xT, wgt2, wa, wb_words, wb_scales, wd_words, wd_scales, b, offs, offs2, out):
    nc = tc.nc
    with ExitStack() as ctx:
        keep = ctx.enter_context(tc.tile_pool(name="keep", bufs=1))
        laid = ctx.enter_context(tc.tile_pool(name="laid", bufs=1))
        psum = ctx.enter_context(tc.psum_pool(name="psum", bufs=1))

        def tile(shape, dtype, name, slot=""):
            return keep.tile(shape, dtype, name=name, tag=slot or name, align_bytes=64)

        def tile_at(kib, shape, dtype, name):
            return laid.tile(shape, dtype, name=name, offset=int(kib * KIB), align_bytes=64)

        def bank_tile(shape, number):
            return psum.tile(shape, F32, name="bank%d" % number)

        def mx(out_ap, w_words, w_scales, a_words, a_scales):
            nc.tensor.matmul_mx(
                out=out_ap,
                lhsT=w_words.bitcast(FP8X4),
                lhsT_scale=w_scales,
                rhs=a_words.bitcast(FP8X4),
                rhs_scale=a_scales,
                start=True,
                stop=True,
            )

        tab_list = keep.tile([P, J // 16], U16, name="tab_list")
        head_lists = keep.tile([P, J // 16], U16, name="head_lists")
        tab_s = tile([P, T], U8, "tab_s")
        tab_w = tile([P, T], I32, "tab_w", "slot_tab")
        wb_w = tile([P, R], I32, "wb_w", "slot_wb")
        wb_s = tile_at(25, [P, R], U8, "wb_s")
        wgt = tile([P, J], F32, "wgt")
        head_w = tile([P, P], F32, "head_w")
        identity = tile([P, P], F32, "identity")
        x_rows = xT.rearrange("(p i) t -> i p t", i=PACK)

        nc.gpsimd.memset(tab_s[:STAGE, :].bitcast(I32), 0)
        nc.gpsimd.memset(wb_s[:STAGE, :].bitcast(I32), 0)
        make_identity(nc, identity[:])
        nc.gpsimd.memset(head_w[HEADS * RUN :, :], 0.0)

        nc.sync.dma_start(tab_list[:], offs)
        nc.scalar.dma_start(out=tab_s[STAGE:P, :].bitcast(I32), in_=tab_scales[0].bitcast(I32))
        nc.sync.dma_start(out=head_w[: HEADS * RUN, :], in_=wgt2.rearrange("p (h v) -> (p h) v", h=2)[::17].rearrange("a (u v) -> a u v", v=P))
        nc.scalar.dma_start(out=wb_s[STAGE:P, :].bitcast(I32), in_=wb_scales[0].bitcast(I32))
        nc.sync.dma_start(out=tab_w[:], in_=words_of(tab_words))
        nc.sync.dma_start(head_lists[:], offs2)
        nc.sync.dma_start(out=wb_w[:], in_=words_of(wb_words))
        x_plane = [tile_at(4, [P, T], F32, "x_plane0")]
        nc.sync.dma_start(out=x_plane[0][:], in_=x_rows[0])

        spread = tile([P, RUN, P], F32, "spread")
        by_token = bank_tile([P, P], 5)
        nc.tensor.transpose(by_token[:], head_w[:], identity[:])
        nc.scalar.copy(
            out=spread[:].rearrange("v u (g s) -> v u g s", s=16),
            in_=by_token[:, : HEADS * RUN].rearrange("v (g u) -> v u g", u=RUN).unsqueeze(3).to_broadcast([P, RUN, HEADS, 16]),
        )
        for u in range(RUN // PACK):
            turned = bank_tile([P, PACK, SUB], 6 + u)
            for c in range(PACK):
                nc.tensor.transpose(turned[:, c, :], spread[:, PACK * u + c, :], identity[:])
            nc.scalar.copy(out=wgt[:, u * PACK * P : (u + 1) * PACK * P], in_=turned[:].rearrange("p c v -> p (c v)"))

        v_rows = tile_at(24, [P, J], U8, "v_rows")
        halves = [slice(h * J // 2, (h + 1) * J // 2) for h in range(2)]
        for h in range(2):
            nc.vector.tensor_copy(v_rows[:, halves[h]], tab_s[:].indirect(tab_list[:, h * J // 32 : (h + 1) * J // 32]))
        both_rows = tile_at(34, [P, J + R], U8, "both_rows")
        for h in range(2):
            nc.vector.tensor_copy(both_rows[96:P, halves[h]].bitcast(I32), v_rows[96:P, halves[h]].bitcast(I32))
        nc.gpsimd.tensor_copy(
            out=both_rows[:, J:].rearrange("p (t c i) -> p c t i", t=PACK, i=16),
            in_=wb_s[:].rearrange("p (c i t) -> p c t i", t=PACK, i=16),
        )
        both_s = tile([P, J + R], U8, "both_s")
        place_scale_rows((nc.sync,), both_s, both_rows[STAGE:P, :])
        v_s = both_s[:, :J]
        wbp_s = both_s[:, J:]
        x_plane.append(tile_at(17.25, [P, T], F32, "x_plane1"))
        nc.sync.dma_start(out=x_plane[1][:], in_=x_rows[1])

        v_w = [tile([P, J // 2], U32, "v_w0"), tile_at(47.5, [P, J // 2], U32, "v_w1")]
        for h in range(2):
            nc.vector.tensor_copy(v_w[h][:], tab_w[:].bitcast(U32).indirect(tab_list[:, h * J // 32 : (h + 1) * J // 32]))
        x_plane.append(tile_at(25.25, [P, T], F32, "x_plane2"))
        nc.sync.dma_start(out=x_plane[2][:], in_=x_rows[2])

        wbp_w = tile([P, R], I32, "wbp_w")
        nc.gpsimd.tensor_copy(
            out=wbp_w[:].rearrange("p (t c i) -> p c t i", t=PACK, i=4),
            in_=wb_w[:].rearrange("p (c i t) -> p c t i", t=PACK, i=4),
        )

        def first_layer(number, w_words, w_scales, a_words, a_scales):
            acc = bank_tile([P, PACK, SUB], number)
            for t in range(PACK):
                rows = slice(t * P, (t + 1) * P)
                mx(acc[:, t, :], w_words[:, rows], w_scales[:, rows], a_words, a_scales)
            return acc

        yb = []
        for s in range(J // SUB):
            cols = slice(s * SUB, (s + 1) * SUB)
            acc = first_layer(s % RING, wbp_w, wbp_s, v_w[s // RING][:, s % RING * SUB : (s % RING + 1) * SUB], v_s[:, cols])
            yb.append(tile([P, SUB, PACK], F32, "yb%d" % s))
            nc.scalar.activation(out=yb[s][:], in_=acc[:].rearrange("p t c -> p c t"), func=IDENTITY)

        picked = tile([P, PACK * J], F32, "picked")[:]
        wa_bf = [
            None,
            picked[:, 3 * J :].bitcast(BF16).rearrange("p (c w) -> p c w", c=CHUNKS)[:, 0 : CHUNKS : CHUNKS - 1],
        ]

        def gather(i, lo, hi):
            nc.vector.tensor_tensor(
                picked[:, i * J + lo : i * J + hi],
                x_plane[i][:].indirect(head_lists[:, lo // 16 : hi // 16]),
                wgt[:, lo:hi],
                MULT,
            )

        x_bf = {}
        x_w = [tile([P, CHUNK], U32, "x_w%d" % c) for c in range(CHUNKS)]
        x_s = [tile([P, CHUNK], U8, "x_s%d" % c) for c in range(CHUNKS)]

        def weave_x(piece, first, count, skip=0):
            lo, hi = PIECES[piece]
            nc.scalar.copy(
                out=x_bf[piece].rearrange("p (c i t) -> p c t i", t=PACK, i=4)[:, skip // 4 :, first : first + count],
                in_=picked.rearrange("p (t c i) -> p c t i", t=PACK, i=4)[:, (lo + skip) // 4 : hi // 4, first : first + count],
            )

        def quantize_x(piece):
            lo, hi = PIECES[piece]
            c = lo // CHUNK
            cols = slice(lo - c * CHUNK, hi - c * CHUNK)
            nc.vector.quantize_mx(out=x_w[c][:, cols].bitcast(FP8X4), scales=x_s[c][:, cols], in_=x_bf[piece])

        x_plane.append(tile_at(35, [P, T], F32, "x_plane3"))
        nc.sync.dma_start(out=x_plane[3][:], in_=x_rows[3])
        gather(0, 0, J)
        bias_rows = tile_at(4, [P, P], F32, "bias_rows")
        nc.gpsimd.memset(bias_rows[: P - PACK, :], 0.0)
        nc.sync.dma_start(out=bias_rows[P - PACK :, :], in_=b.rearrange("(t p) -> t p", p=P))
        wa_raw = tile_at(8, [P, PACK, R], F32, "wa_raw")
        nc.sync.dma_start(out=wa_raw[:], in_=wa.rearrange("(p i) r -> p i r", i=PACK))
        gather(1, 0, J)
        for piece, (lo, hi) in enumerate(PIECES[: EARLY + 1]):
            x_bf[piece] = tile_at(46 + lo // SUB, [P, (hi - lo) * PACK], BF16, "x_bf%d" % piece)[:]
            weave_x(piece, 0, 2)
        gather(2, 0, J)
        wd_w = tile_at(18, [P, N], I32, "wd_w")
        nc.sync.dma_start(out=wd_w[:], in_=words_of(wd_words))
        gather(3, 0, CHUNK)
        gather(3, CHUNK, 3 * CHUNK)
        bias = tile([P, N // P], F32, "bias")
        bias_turned = bank_tile([P, P], 7)
        nc.tensor.transpose(bias_turned[:], bias_rows[:], identity[:])
        nc.scalar.copy(out=bias[:], in_=bias_turned[:, P - PACK :])
        wd_s = tile_at(21, [P, N], U8, "wd_s")
        place_scale_rows((nc.sync,), wd_s, wd_scales[0])

        def round_wa(copy, rounded, h, channels):
            copy(
                out=rounded.rearrange("p t (m i) -> p m i t", i=PACK),
                in_=wa_raw[:].rearrange("p i (m t) -> p m i t", t=PACK)[:, channels, :, 2 * h : 2 * h + 2],
            )

        weave_x(0, 2, 2)
        quantize_x(0)
        wa_low = [tile([P, 2, R // 2], BF16, "wa_low%d" % u) for u in range(2)]
        for u in range(2):
            round_wa(nc.vector.tensor_copy, wa_low[u][:], 0, slice(u * P // 2, (u + 1) * P // 2))
        round_wa(nc.scalar.copy, wa_bf[1], 1, slice(0, P))
        weave_x(1, 2, 2)
        weave_x(2, 2, 2)
        wa_s = tile([P, R], U8, "wa_s")
        wa_w = tile([P, R], U32, "wa_w")
        for u in range(2):
            for t in range(2):
                cols = slice(t * P + u * P // 2, t * P + (u + 1) * P // 2)
                nc.vector.quantize_mx(out=wa_w[:, cols].bitcast(FP8X4), scales=wa_s[:, cols], in_=wa_low[u][:, t, :])
        for t in (2, 3):
            cols = slice(t * P, (t + 1) * P)
            nc.vector.quantize_mx(out=wa_w[:, cols].bitcast(FP8X4), scales=wa_s[:, cols], in_=wa_bf[1][:, t - 2, :])

        ya = {}
        ya_share = {}

        def project_x(s):
            cols = slice(s % 2 * SUB, (s % 2 + 1) * SUB)
            ya[s] = first_layer(YA_BANKS[s], wa_w, wa_s, x_w[s // 2][:, cols], x_s[s // 2][:, cols])

        def copy_share(c):
            ya_share[c] = tile([P, SHARE, PACK], F32, "ya_share%d" % c)
            nc.scalar.activation(out=ya_share[c][:], in_=ya[2 * c][:, :, SUB - SHARE :].rearrange("p t c -> p c t"), func=IDENTITY)


        project_x(0)
        project_x(1)
        gather(3, 3 * CHUNK, J)
        quantize_x(1)
        project_x(2)
        quantize_x(2)
        project_x(3)
        x_bf[3] = tile_at(8, [P, CHUNK * PACK], BF16, "x_bf3")[:]
        weave_x(3, 0, PACK)
        copy_share(1)
        x_bf[4] = tile_at(49.5, [P, CHUNK * PACK], BF16, "x_bf4")[:]
        nc.gpsimd.tensor_scalar(
            x_bf[4][:, : HELP * PACK].rearrange("p (c t) -> p c t", t=PACK),
            picked.rearrange("p (t c) -> p c t", t=PACK)[:, 3 * CHUNK : 3 * CHUNK + HELP],
            1.0,
            0.0,
            MULT,
            ADD,
        )
        weave_x(4, 0, PACK, HELP)

        out_rows = out.rearrange("(t p) j -> p t j", p=P)
        h_bf = {}
        h_w = [tile([P, SUB], U32, "h_w%d" % s) for s in range(J // SUB)]
        h_s = [tile([P, SUB], U8, "h_s%d" % s) for s in range(J // SUB)]

        def product(s, slot, tokens):
            h_bf[s] = tile_at(slot, [P, SUB, PACK], BF16, "h_bf%d" % s)
            if tokens < SUB:
                nc.gpsimd.tensor_tensor(h_bf[s][:, tokens:], ya_share[s // 2][:], yb[s][:, tokens:], MULT)
            nc.vector.tensor_tensor(h_bf[s][:, :tokens], ya[s][:, :, :tokens].rearrange("p t c -> p c t"), yb[s][:, :tokens], MULT)

        def second_layer(order, numbers):
            a_bank = N // P // len(numbers)
            banks = [bank_tile([P, a_bank, CHUNK], number) for number in numbers]
            for s in order:
                nc.vector.quantize_mx(out=h_w[s][:].bitcast(FP8X4), scales=h_s[s][:], in_=h_bf[s][:].rearrange("p c t -> p (c t)"))
                for t in range(N // P):
                    rows = slice(t * P, (t + 1) * P)
                    mx(banks[t // a_bank][:, t % a_bank, s % 2 * SUB : (s % 2 + 1) * SUB], wd_w[:, rows], wd_s[:, rows], h_w[s][:], h_s[s][:])
            return [banks[t // a_bank][:, t % a_bank, :] for t in range(N // P)]

        def empty_and_store(c, t, bank, on_scalar, queue):
            result = tile([P, CHUNK], F32, "result%d_%d" % (c, t))
            if on_scalar:
                nc.scalar.activation(out=result[:], in_=bank, func=IDENTITY, bias=bias[:, t : t + 1])
            else:
                nc.vector.tensor_scalar(result[:], bank, bias[:, t : t + 1], None, ADD)
            queue.dma_start(out=out_rows[:, t, c * CHUNK : (c + 1) * CHUNK], in_=result[:])

        last = CHUNKS - 1
        for c in range(CHUNKS):
            order = (2 * c + 1, 2 * c) if c else (0, 1)
            product(order[0], H_KIB[c], SUB)
            product(order[1], H_KIB[c - 1], SUB - SHARE if c else SUB)
            ahead = c + EARLY
            if ahead < CHUNKS:
                quantize_x(ahead + 1)
                project_x(2 * ahead)
            banks = second_layer(order, OUT_BANKS[c])
            if ahead < CHUNKS:
                copy_share(ahead)
                project_x(2 * ahead + 1)
            for t, bank in enumerate(banks):
                empty_and_store(c, t, bank, c < last or t % 2 == 1, nc.sync)
